import numpy as np
import ml_dtypes


def mxq(x, axis, fmt="e4m3"):
    dtype, down = {"e4m3": (ml_dtypes.float8_e4m3fn, 7), "e5m2": (ml_dtypes.float8_e5m2, 14)}[fmt]
    v = np.moveaxis(np.asarray(x, np.float32).astype(ml_dtypes.bfloat16).astype(np.float64), axis, -1)
    blocks = v.reshape(v.shape[:-1] + (-1, 32))
    amax = np.abs(blocks).max(-1, keepdims=True)
    byte = np.maximum(np.where(amax > 0, np.frexp(amax)[1] - 1 + 127, 0) - down, 1)
    scale = np.exp2(byte - 127.0)
    codes = (blocks / scale).astype(np.float32).astype(dtype).astype(np.float64)
    return np.moveaxis((codes * scale).reshape(v.shape), -1, axis)


WIDE = False


def mx_kscale(k):
    if not WIDE:
        return np.ones(k)
    levels = np.array([10, -10, 5, -5, 0])
    if k % 512:
        return np.exp2(np.random.permutation(np.resize(levels, k // 32))).repeat(32)
    a = np.empty((k // 512, 16))
    for p in range(k // 512):
        a[p, :8] = np.random.permutation(np.resize(levels, 8))
        for g in range(8):
            far = levels[np.abs(levels - a[p, g]) >= 10]
            a[p, g + 8] = far[np.random.randint(len(far))]
    return np.exp2(a.ravel()).repeat(32)


BF16 = ml_dtypes.bfloat16


def bf(x):
    return np.asarray(x, np.float32).astype(BF16)


def f64(x):
    return np.asarray(x).astype(np.float64)

def planes(Y):
    n, m = Y.shape
    b = f64(bf(Y)).reshape(n // 32, 32, m)
    amax = np.abs(b).max(1)
    byte = np.clip(np.where(amax > 0, np.frexp(amax)[1] - 1 + 127 - 7, 1), 1, 254)
    codes = (b * np.exp2(127.0 - byte)[:, None, :]).reshape(n, m).astype(np.float32).astype(ml_dtypes.float8_e4m3fn).view(np.uint8)
    words = codes.reshape(n // 512, 128, 4, m).transpose(0, 1, 3, 2)
    return np.ascontiguousarray(words), np.ascontiguousarray(byte.astype(np.uint8).reshape(n // 512, 16, m))


B, X, F = 1024, 1024, 1024
N = X // 2


def setup_inputs():
    s, t = mx_kscale(X), mx_kscale(F)
    return {
        "z": bf(np.random.standard_normal((B, X))),
        "ctrl": bf(np.random.standard_normal((B, N)) * 0.5),
        "c": bf((1.0 + 0.1 * np.random.standard_normal(X)) * s),
        "w1": bf(np.random.standard_normal((X, F)) / np.sqrt(X) / s[:, None] / t[None, :]),
        "g": bf((1.0 + 0.1 * np.random.standard_normal(F)) * t),
        "b1": bf(np.random.standard_normal(F) * 0.4),
        "damp": bf(np.random.uniform(0.1, 0.6, N)),
    }


def hamiltonian_gradient(z, c, w1, g, b1):
    x = c[None, :] * z
    m = mxq(x, 1, "e4m3") @ mxq(w1, 0, "e4m3")
    th = np.tanh(g[None, :] * m + b1[None, :])
    delta = g[None, :] * th
    r = mxq(delta, 1, "e4m3") @ mxq(w1.T, 0, "e4m3")
    return c[None, :] * r


def core(z, ctrl, c, w1, g, b1, damp):
    n = damp.shape[0]
    grad = hamiltonian_gradient(f64(z), f64(c), f64(w1), f64(g), f64(b1))
    hq = grad[:, :n]
    hp = grad[:, n:]
    dq = hp
    dp = -hq - f64(damp)[None, :] * hp + f64(ctrl)
    return np.concatenate([dq, dp], axis=-1)


def reference(z, ctrl, c, w1, g, b1, damp):
    R_out = core(z, ctrl, c, w1, g, b1, damp)
    words, scales = planes(R_out)
    return R_out, words, scales

@@ -1,0 +1,520 @@
+from contextlib import ExitStack
+
+import concourse.mybir as mybir
+from concourse.masks import make_identity
+
+F32 = mybir.dt.float32
+BF16 = mybir.dt.bfloat16
+I32 = mybir.dt.int32
+U32 = mybir.dt.uint32
+U8 = mybir.dt.uint8
+FP8X4 = mybir.dt.float8_e4m3fn_x4
+ALU = mybir.AluOpType
+ACT = mybir.ActivationFunctionType
+
+B, X, F = 1024, 1024, 1024
+N = X // 2
+P = 128
+PACK = 4
+GROUP = P * PACK
+FLOPS = 4 * B * X * F
+
+
+def tile_porthamiltoniannetfield_x1_kernel(tc, z, ctrl, c, w1, g, b1, damp, out_0, out_1, out_2):
+    nc = tc.nc
+    with ExitStack() as ctx:
+        keep = ctx.enter_context(tc.tile_pool(name="keep", bufs=1))
+        work = ctx.enter_context(tc.tile_pool(name="work", bufs=2))
+        psum = ctx.enter_context(tc.psum_pool(name="psum", bufs=4))
+        ctx.enter_context(tc.manual_schedule())
+
+        T = {}
+
+        def kept(key, shape, dtype):
+            name = "_".join([str(k) for k in key])
+            T[key] = keep.tile(shape, dtype, name=name, align_bytes=64)
+            return T[key]
+
+        def rot(key, shape, dtype, bufs):
+            name = "_".join([str(k) for k in key])
+            T[key] = work.tile(shape, dtype, name=name, tag=key[0], bufs=bufs, align_bytes=64)
+            return T[key]
+
+        def bank(key, tag):
+            name = "_".join([str(k) for k in key])
+            T[key] = psum.tile([P, GROUP], F32, name=name, tag=tag)
+            return T[key]
+
+        def load_z(gb, gx, t0, t1):
+            if ("z", gb, gx) not in T:
+                kept(("z", gb, gx), [P, PACK, GROUP], BF16)
+            src = z[GROUP * gb : GROUP * (gb + 1), GROUP * gx : GROUP * (gx + 1)].rearrange("(p t) x -> p t x", t=PACK)
+            nc.sync.dma_start(out=T[("z", gb, gx)][:, t0:t1, :], in_=src[:, t0:t1, :])
+
+        def load_w(gx, gf):
+            t = kept(("w", gx, gf), [P, PACK, GROUP], BF16)
+            nc.sync.dma_start(out=t[:], in_=w1[GROUP * gx : GROUP * (gx + 1), GROUP * gf : GROUP * (gf + 1)].rearrange("(p j) f -> p j f", j=PACK))
+
+        def load_ctrl(gb):
+            t = kept(("ctrl", gb), [P, PACK, N], BF16)
+            nc.sync.dma_start(out=t[:], in_=ctrl[GROUP * gb : GROUP * (gb + 1), :].rearrange("(p t) n -> p t n", t=PACK))
+
+        def load_vec(name, vec):
+            t = kept((name,), [P, 2, PACK], BF16)
+            nc.scalar.dma_start(out=t[:], in_=vec.rearrange("(g p t) -> p g t", g=2, t=PACK))
+
+        def mx_tiles(key, width):
+            kept(("q",) + key, [P, width], U32)
+            kept(("s",) + key, [P, width], U8)
+
+        def quantize(key, src, lo, hi):
+            nc.vector.quantize_mx(out=T[("q",) + key][:, lo:hi].bitcast(FP8X4), scales=T[("s",) + key][:, lo:hi], in_=src)
+
+        def mx_pass(out, lkey, l0, rkey, first):
+            nc.tensor.matmul_mx(
+                out=out,
+                lhsT=T[("q",) + lkey][:, l0 : l0 + P].bitcast(FP8X4),
+                lhsT_scale=T[("s",) + lkey][:, l0 : l0 + P],
+                rhs=T[("q",) + rkey][:].bitcast(FP8X4),
+                rhs_scale=T[("s",) + rkey][:],
+                start=first,
+                stop=not first,
+            )
+
+        def lay(o, i, eng):
+            if eng == "v":
+                nc.vector.tensor_copy(out=o, in_=i)
+            elif eng == "s":
+                nc.scalar.copy(out=o, in_=i)
+            else:
+                nc.gpsimd.tensor_scalar(out=o, in0=i, scalar1=1.0, scalar2=0.0, op0=ALU.mult, op1=ALU.add)
+
+        def z_turn(gb, gx, h):
+            bk = bank(("zt", gb, gx, h), "tr")
+            words = T[("z", gb, gx)][:].rearrange("p t x -> p (t x)").bitcast(F32)
+            for u in range(2):
+                for tt in range(2):
+                    w0 = (2 * h + tt) * 256
+                    nc.tensor.transpose(bk[:, (2 * u + tt) * P : (2 * u + tt + 1) * P], words[:, w0 + u : w0 + 256 : 2], ident[:])
+
+        def x_mul(gb, gx, h):
+            if ("xg", gb, gx) not in T:
+                rot(("xg", gb, gx), [P, GROUP * PACK], BF16, 2)
+            nc.vector.tensor_tensor(
+                out=T[("xg", gb, gx)][:, 1024 * h : 1024 * (h + 1)].rearrange("p (r u e) -> p r u e", u=2, e=2),
+                in0=T[("zt", gb, gx, h)][:].bitcast(BF16).rearrange("p (u r e) -> p r u e", u=2, e=2),
+                in1=T[("c4",)][:, gx, :].rearrange("p (u e) -> p u e", e=2).unsqueeze(1).to_broadcast([P, 256, 2, 2]),
+                op=ALU.mult,
+            )
+
+        def x_q(gb, gx):
+            mx_tiles(("x", gb, gx), GROUP)
+            quantize(("x", gb, gx), T[("xg", gb, gx)][:], 0, GROUP)
+
+        def wa_lay(gx, gf, h, eng):
+            if ("wa", gx, gf) not in T:
+                rot(("wa", gx, gf), [P, GROUP * PACK], BF16, 3)
+                mx_tiles(("wa", gx, gf), GROUP)
+            o = T[("wa", gx, gf)][:].rearrange("p (t m j) -> p t m j", t=PACK, j=PACK)[:, 2 * h : 2 * h + 2]
+            i = T[("w", gx, gf)][:].rearrange("p j (m t) -> p t m j", t=PACK)[:, 2 * h : 2 * h + 2]
+            lay(o, i, eng)
+
+        def wa_q(gx, gf, h):
+            quantize(("wa", gx, gf), T[("wa", gx, gf)][:, 1024 * h : 1024 * (h + 1)], 256 * h, 256 * (h + 1))
+
+        def wb_turn(gx, gf, h):
+            bk = bank(("wt", gx, gf, h), "tr")
+            words = T[("w", gx, gf)][:].rearrange("p j f -> p (j f)").bitcast(F32)
+            for jj in range(2):
+                for u in range(2):
+                    w0 = (2 * h + jj) * 256
+                    nc.tensor.transpose(bk[:, (2 * jj + u) * P : (2 * jj + u + 1) * P], words[:, w0 + u : w0 + 256 : 2], ident[:])
+
+        def wb_out(gx, gf, h):
+            if ("wb", gx, gf) not in T:
+                rot(("wb", gx, gf), [P, GROUP * PACK], BF16, 2)
+            nc.scalar.copy(
+                out=T[("wb", gx, gf)][:].bitcast(F32).rearrange("p (r h q) -> p r h q", h=2, q=4)[:, :, h, :],
+                in_=T[("wt", gx, gf, h)][:].rearrange("p (q r) -> p r q", q=4),
+            )
+
+        def wb_q(gx, gf):
+            mx_tiles(("wb", gx, gf), GROUP)
+            quantize(("wb", gx, gf), T[("wb", gx, gf)][:], 0, GROUP)
+
+        def s1_mm(gb, gf, t):
+            bk = bank(("m", gb, gf, t), "mm")
+            for gx in range(2):
+                mx_pass(bk[:], ("wa", gx, gf), t * P, ("x", gb, gx), gx == 0)
+
+        def s1_tanh(gb, gf, t):
+            if ("th", gb, gf) not in T:
+                rot(("th", gb, gf), [P, PACK, GROUP], F32, 2)
+            nc.scalar.activation(
+                out=T[("th", gb, gf)][:, t, :], in_=T[("m", gb, gf, t)][:], func=ACT.Tanh,
+                bias=T[("b32",)][:, gf, t : t + 1], scale=T[("g32",)][:, gf, t : t + 1],
+            )
+
+        def d_mul(gb, gf, h):
+            if ("dg", gb, gf) not in T:
+                rot(("dg", gb, gf), [P, GROUP * PACK], BF16, 2)
+            nc.vector.tensor_tensor(
+                out=T[("dg", gb, gf)][:, 1024 * h : 1024 * (h + 1)].rearrange("p (c i t) -> p c t i", i=4, t=PACK),
+                in0=T[("th", gb, gf)][:, :, 256 * h : 256 * (h + 1)].rearrange("p t (c i) -> p c t i", i=4),
+                in1=T[("g32",)][:, gf, :].unsqueeze(1).unsqueeze(3).to_broadcast([P, 64, PACK, 4]),
+                op=ALU.mult,
+            )
+
+        def d_q(gb, gf):
+            mx_tiles(("d", gb, gf), GROUP)
+            quantize(("d", gb, gf), T[("dg", gb, gf)][:], 0, GROUP)
+
+        def s2_mm(gb, gx, i):
+            bk = bank(("r", gb, gx, i), "mm")
+            for gf in range(2):
+                mx_pass(bk[:], ("wb", gx, gf), i * P, ("d", gb, gf), gf == 0)
+
+        def s2_hp(gb, i):
+            hp = rot(("hp", gb, i), [P, GROUP], F32, 3)
+            nc.scalar.activation(out=hp[:], in_=T[("r", gb, 1, i)][:], func=ACT.Copy, scale=cn[:, 4 + i : 5 + i])
+
+        def s2_v(gb, i, eng):
+            v = rot(("v", gb, i), [P, GROUP], F32, 3)
+            if eng == "s":
+                nc.scalar.activation(out=v[:], in_=T[("r", gb, 1, i)][:], func=ACT.Copy, scale=ndc[:, i : i + 1])
+            elif eng == "v":
+                nc.vector.tensor_scalar(out=v[:], in0=T[("hp", gb, i)][:], scalar1=nd[:, i : i + 1], scalar2=None, op0=ALU.mult)
+            else:
+                nc.gpsimd.tensor_scalar(out=v[:], in0=T[("hp", gb, i)][:], scalar1=nd[:, i : i + 1], scalar2=0.0, op0=ALU.mult, op1=ALU.add)
+
+        def s2_stt(gb, i):
+            w = rot(("wv", gb, i), [P, GROUP], F32, 3)
+            nc.vector.scalar_tensor_tensor(out=w[:], in0=T[("r", gb, 0, i)][:], scalar=ncl[:, i : i + 1], in1=T[("v", gb, i)][:], op0=ALU.mult, op1=ALU.add)
+
+        def s2_turn(key, gb, i):
+            bk = bank(("t" + key, gb, i), "tr")
+            for t in range(PACK):
+                nc.tensor.transpose(bk[:, t * P : (t + 1) * P], T[(key, gb, i)][:, t * P : (t + 1) * P], ident[:])
+
+        def s2_dq(gb, i, eng):
+            lay(T[("y", gb)][:, :, i * P : (i + 1) * P], T[("thp", gb, i)][:].rearrange("p (t n) -> p t n", t=PACK), eng)
+
+        def s2_dp(gb, i):
+            nc.vector.tensor_tensor(
+                out=T[("y", gb)][:, :, N + i * P : N + (i + 1) * P],
+                in0=T[("twv", gb, i)][:].rearrange("p (t n) -> p t n", t=PACK),
+                in1=T[("ctrl", gb)][:, :, i * P : (i + 1) * P],
+                op=ALU.add,
+            )
+
+        def y_lay(gb, n0, n1, eng):
+            o = T[("yb", gb)][:, PACK * n0 : PACK * n1].rearrange("p (c i t) -> p c t i", i=4, t=PACK)
+            i = T[("y", gb)][:, :, n0:n1].rearrange("p t (c i) -> p c t i", i=4)
+            lay(o, i, eng)
+
+        def y_q(gb, n0, n1):
+            quantize(("y", gb), T[("yb", gb)][:, PACK * n0 : PACK * n1], n0, n1)
+
+        def y_store(gb, n0, n1):
+            nc.sync.dma_start(
+                out=out_0[GROUP * gb : GROUP * (gb + 1), n0:n1].rearrange("(p t) n -> p t n", t=PACK), in_=T[("y", gb)][:, :, n0:n1]
+            )
+
+        def q_store(gb, n0, n1):
+            nc.sync.dma_start(
+                out=out_1[gb].rearrange("p m t -> p (m t)").bitcast(I32)[:, n0:n1], in_=T[("q", "y", gb)][:, n0:n1].bitcast(I32)
+            )
+
+        def s_store(gb, q, eng):
+            (nc.sync if eng == "y" else nc.scalar).dma_start(
+                out=out_2[gb, 4 * q : 4 * q + 4, :].bitcast(I32), in_=T[("s", "y", gb)][32 * q : 32 * q + 4, :].bitcast(I32)
+            )
+
+        warm = kept(("warm",), [P, 8], F32)
+        ident = kept(("ident",), [P, P], F32)
+        rows = kept(("rows",), [P, P], BF16)
+        rows32 = kept(("rows32",), [P, P], F32)
+        cn = kept(("cn",), [P, 12], F32)
+        ncl = kept(("ncl",), [P, 4], F32)
+        ndc = kept(("ndc",), [P, 4], F32)
+        kept(("g32",), [P, 2, PACK], F32)
+        kept(("b32",), [P, 2, PACK], F32)
+
+        nd = kept(("nd",), [P, 4], F32)
+        for gb in range(2):
+            kept(("y", gb), [P, PACK, X], F32)
+            kept(("yb", gb), [P, X * PACK], BF16)
+            mx_tiles(("y", gb), X)
+
+        def setup():
+            load_vec("c4", c)
+            load_vec("g4", g)
+            load_vec("b4", b1)
+            nc.vector.memset(warm[:], 0.0)
+            nc.scalar.activation(out=warm[:, 4:5], in_=warm[:, 0:1], func=ACT.Tanh)
+            make_identity(nc, ident[:])
+            nc.gpsimd.memset(rows[:], 0.0)
+
+        def load_rows():
+            nc.sync.dma_start(out=rows[0:8, :], in_=c.rearrange("(i p) -> i p", p=P))
+            nc.sync.dma_start(out=rows[8:12, :], in_=damp.rearrange("(i p) -> i p", p=P))
+
+        def consts_a():
+            nc.vector.tensor_copy(out=T[("g32",)][:], in_=T[("g4",)][:])
+            nc.vector.tensor_copy(out=T[("b32",)][:], in_=T[("b4",)][:])
+
+        def consts_b0():
+            nc.scalar.copy(out=rows32[:], in_=rows[:])
+
+        def consts_b():
+            bk = bank(("rowt",), "tr")
+            nc.tensor.transpose(bk[:, 0:P], rows32[:], ident[:])
+
+        def consts_c():
+            nc.vector.tensor_copy(out=cn[:], in_=T[("rowt",)][:, 0:12])
+
+        def consts_d():
+            nc.vector.tensor_scalar(out=ncl[:], in0=cn[:, 0:4], scalar1=-1.0, scalar2=None, op0=ALU.mult)
+            nc.vector.tensor_scalar(out=nd[:], in0=cn[:, 8:12], scalar1=-1.0, scalar2=None, op0=ALU.mult)
+            nc.vector.scalar_tensor_tensor(out=ndc[:], in0=cn[:, 4:8], scalar=-1.0, in1=cn[:, 8:12], op0=ALU.mult, op1=ALU.mult)
+
+        load_w(0, 0)
+        setup()
+        wa_lay(0, 0, 0, "v")
+        consts_a()
+        wb_turn(0, 0, 0)
+        load_z(0, 1, 2, 4)
+        z_turn(0, 1, 1)
+        load_w(0, 1)
+        wa_q(0, 0, 0)
+        load_w(1, 0)
+        wb_turn(0, 0, 1)
+        wa_lay(0, 0, 1, "s")
+        wb_out(0, 0, 0)
+        wa_lay(0, 1, 0, "s")
+        wb_turn(0, 1, 1)
+        load_z(0, 0, 2, 4)
+        load_z(0, 0, 0, 2)
+        load_z(0, 1, 0, 2)
+        z_turn(0, 0, 1)
+        wa_q(0, 0, 1)
+        load_w(1, 1)
+        load_z(1, 0, 0, 4)
+        wa_lay(0, 1, 1, "v")
+        x_mul(0, 1, 1)
+        wb_out(0, 0, 1)
+        wa_lay(1, 0, 1, "v")
+        wa_q(0, 1, 1)
+        z_turn(0, 1, 0)
+        wb_out(0, 1, 1)
+        wa_lay(1, 0, 0, "s")
+        z_turn(0, 0, 0)
+        wa_q(1, 0, 1)
+        wa_q(0, 1, 0)
+        wb_q(0, 0)
+        wa_lay(1, 1, 1, "s")
+        wb_turn(0, 1, 0)
+        x_mul(0, 0, 1)
+        load_z(1, 1, 0, 4)
+        wb_turn(1, 1, 0)
+        x_mul(0, 1, 0)
+        wb_out(0, 1, 0)
+        load_rows()
+        wb_out(1, 1, 0)
+        x_mul(0, 0, 0)
+        wa_q(1, 0, 0)
+        x_q(0, 0)
+        x_q(0, 1)
+        z_turn(1, 0, 0)
+        wa_lay(1, 1, 0, "s")
+        z_turn(1, 0, 1)
+        z_turn(1, 1, 0)
+        z_turn(1, 1, 1)
+        s1_mm(0, 0, 1)
+        wb_q(0, 1)
+        s1_tanh(0, 0, 1)
+        s1_mm(0, 0, 3)
+        load_ctrl(1)
+        s1_mm(0, 0, 0)
+        s1_tanh(0, 0, 3)
+        x_mul(1, 1, 0)
+        wa_q(1, 1, 0)
+        s1_mm(0, 0, 2)
+        x_mul(1, 1, 1)
+        s1_tanh(0, 0, 0)
+        wa_q(1, 1, 1)
+        s1_tanh(0, 0, 2)
+        s1_mm(0, 1, 1)
+        s1_mm(0, 1, 3)
+        x_mul(1, 0, 1)
+        x_mul(1, 0, 0)
+        s1_mm(0, 1, 0)
+        s1_mm(0, 1, 2)
+        x_q(1, 1)
+        consts_b0()
+        wb_turn(1, 1, 1)
+        x_q(1, 0)
+        d_mul(0, 0, 1)
+        s1_tanh(0, 1, 1)
+        wb_turn(1, 0, 0)
+        wb_turn(1, 0, 1)
+        consts_b()
+        s1_tanh(0, 1, 3)
+        s1_mm(1, 0, 1)
+        s1_tanh(0, 1, 0)
+        s1_tanh(0, 1, 2)
+        wb_out(1, 1, 1)
+        d_mul(0, 0, 0)
+        d_mul(0, 1, 0)
+        s1_mm(1, 0, 3)
+        wb_out(1, 0, 0)
+        wb_out(1, 0, 1)
+        d_mul(0, 1, 1)
+        wb_q(1, 0)
+        s1_tanh(1, 0, 1)
+        consts_c()
+        d_q(0, 1)
+        s1_tanh(1, 0, 3)
+        s1_mm(1, 0, 2)
+        s1_mm(1, 1, 0)
+        s1_mm(1, 1, 3)
+        s1_tanh(1, 0, 2)
+        d_q(0, 0)
+        s1_mm(1, 0, 0)
+        consts_d()
+        s1_mm(1, 1, 2)
+        s1_tanh(1, 1, 0)
+        s1_tanh(1, 1, 3)
+        wb_q(1, 1)
+        s1_tanh(1, 0, 0)
+        s1_mm(1, 1, 1)
+        d_mul(1, 0, 1)
+        s1_tanh(1, 1, 2)
+        s2_mm(0, 1, 1)
+        s2_mm(0, 1, 0)
+        d_mul(1, 0, 0)
+        s1_tanh(1, 1, 1)
+        s2_mm(0, 1, 3)
+        s2_mm(0, 0, 1)
+        s2_hp(0, 1)
+        s2_hp(0, 0)
+        s2_v(0, 1, "s")
+        s2_turn("hp", 0, 1)
+        d_mul(1, 1, 1)
+        s2_stt(0, 1)
+        d_mul(1, 1, 0)
+        s2_hp(0, 3)
+        s2_turn("hp", 0, 0)
+        s2_v(0, 0, "s")
+        s2_v(0, 3, "v")
+        s2_dq(0, 1, "s")
+        s2_mm(0, 1, 2)
+        s2_hp(0, 2)
+        s2_turn("hp", 0, 3)
+        y_lay(0, 128, 256, "s")
+        d_q(1, 0)
+        s2_turn("wv", 0, 1)
+        s2_mm(0, 0, 0)
+        s2_dq(0, 3, "s")
+        s2_v(0, 2, "s")
+        d_q(1, 1)
+        s2_dq(0, 0, "s")
+        load_ctrl(0)
+        s2_dp(0, 1)
+        s2_turn("hp", 0, 2)
+        s2_stt(0, 0)
+        s2_mm(0, 0, 2)
+        s2_mm(1, 1, 3)
+        s2_mm(0, 0, 3)
+        y_lay(0, 0, 128, "v")
+        s2_turn("wv", 0, 0)
+        s2_mm(1, 0, 3)
+        s2_hp(1, 3)
+        s2_stt(0, 2)
+        s2_v(1, 3, "v")
+        s2_mm(1, 1, 0)
+        s2_dp(0, 0)
+        s2_stt(0, 3)
+        s2_stt(1, 3)
+        y_lay(0, 640, 768, "s")
+        s2_dq(0, 2, "s")
+        y_q(0, 0, 256)
+        y_lay(0, 384, 512, "s")
+        s2_turn("wv", 0, 2)
+        s2_hp(1, 0)
+        s2_turn("wv", 0, 3)
+        y_store(0, 256, 512)
+        y_lay(0, 256, 384, "v")
+        s2_mm(1, 1, 2)
+        y_store(0, 512, 768)
+        s2_v(1, 0, "s")
+        s2_dp(0, 3)
+        s2_dp(0, 2)
+        y_q(0, 256, 512)
+        y_lay(0, 768, 896, "v")
+        y_lay(0, 512, 640, "s")
+        s2_hp(1, 2)
+        s2_mm(1, 1, 1)
+        y_lay(0, 896, 1024, "s")
+        s2_mm(1, 0, 1)
+        s2_v(1, 2, "v")
+        s2_turn("hp", 1, 3)
+        s2_turn("hp", 1, 2)
+        y_q(0, 768, 1024)
+        y_q(0, 512, 768)
+        s2_dq(1, 3, "s")
+        s2_hp(1, 1)
+        y_store(0, 0, 256)
+        s2_mm(1, 0, 2)
+        s2_dq(1, 2, "v")
+        y_store(0, 768, 1024)
+        y_store(1, 384, 512)
+        y_lay(1, 384, 512, "s")
+        s_store(0, 1, "y")
+        s2_turn("wv", 1, 3)
+        s2_stt(1, 2)
+        s2_mm(1, 0, 0)
+        s2_turn("hp", 1, 0)
+        s2_dp(1, 3)
+        y_lay(1, 256, 384, "s")
+        s2_turn("wv", 1, 2)
+        s2_v(1, 1, "s")
+        s_store(0, 2, "y")
+        s_store(0, 3, "y")
+        q_store(0, 0, 1024)
+        s2_stt(1, 0)
+        s2_dp(1, 2)
+        s2_stt(1, 1)
+        y_store(1, 896, 1024)
+        s2_dq(1, 0, "s")
+        y_store(1, 256, 384)
+        y_q(1, 384, 512)
+        s2_turn("hp", 1, 1)
+        s2_turn("wv", 1, 0)
+        s2_turn("wv", 1, 1)
+        y_q(1, 256, 384)
+        s2_dq(1, 1, "s")
+        s_store(0, 0, "y")
+        s2_dp(1, 0)
+        y_store(1, 768, 896)
+        s2_dp(1, 1)
+        y_lay(1, 768, 896, "s")
+        y_lay(1, 896, 1024, "v")
+        y_lay(1, 640, 768, "v")
+        y_lay(1, 0, 128, "s")
+        y_q(1, 768, 896)
+        y_store(1, 0, 256)
+        y_q(1, 896, 1024)
+        y_lay(1, 512, 640, "s")
+        q_store(1, 256, 512)
+        y_lay(1, 128, 256, "s")
+        y_store(1, 512, 768)
+        q_store(1, 768, 1024)
+        y_q(1, 512, 768)
+        y_q(1, 0, 256)
+        q_store(1, 512, 768)
+        s_store(1, 2, "s")
+        s_store(1, 0, "y")
+        s_store(1, 1, "y")
+        s_store(1, 3, "s")
+        q_store(1, 0, 256)

@@ -45,11 +45,11 @@ def tile_porthamiltoniannetfield_x1_kernel(tc, z, ctrl, c, w1, g, b1, damp, out_
             T[key] = psum.tile([P, GROUP], F32, name=name, tag=tag)
             return T[key]
 
-        def load_z(gb, gx, t0, t1):
-            if ("z", gb, gx) not in T:
-                kept(("z", gb, gx), [P, PACK, GROUP], BF16)
-            src = z[GROUP * gb : GROUP * (gb + 1), GROUP * gx : GROUP * (gx + 1)].rearrange("(p t) x -> p t x", t=PACK)
-            nc.sync.dma_start(out=T[("z", gb, gx)][:, t0:t1, :], in_=src[:, t0:t1, :])
+        def load_z(gb, h):
+            if ("z", gb) not in T:
+                kept(("z", gb), [P, PACK, X], BF16)
+            src = z[GROUP * gb : GROUP * (gb + 1), :].rearrange("(p t) x -> p t x", t=PACK)
+            nc.sync.dma_start(out=T[("z", gb)][:, 2 * h : 2 * h + 2, :], in_=src[:, 2 * h : 2 * h + 2, :])
 
         def load_w(gx, gf):
             t = kept(("w", gx, gf), [P, PACK, GROUP], BF16)
@@ -91,10 +91,10 @@ def tile_porthamiltoniannetfield_x1_kernel(tc, z, ctrl, c, w1, g, b1, damp, out_
 
         def z_turn(gb, gx, h):
             bk = bank(("zt", gb, gx, h), "tr")
-            words = T[("z", gb, gx)][:].rearrange("p t x -> p (t x)").bitcast(F32)
+            words = T[("z", gb)][:].rearrange("p t x -> p (t x)").bitcast(F32)
             for u in range(2):
                 for tt in range(2):
-                    w0 = (2 * h + tt) * 256
+                    w0 = (2 * h + tt) * 512 + gx * 256
                     nc.tensor.transpose(bk[:, (2 * u + tt) * P : (2 * u + tt + 1) * P], words[:, w0 + u : w0 + 256 : 2], ident[:])
 
         def x_mul(gb, gx, h):
@@ -114,13 +114,32 @@ def tile_porthamiltoniannetfield_x1_kernel(tc, z, ctrl, c, w1, g, b1, damp, out_
         def wa_lay(gx, gf, h, eng):
             if ("wa", gx, gf) not in T:
                 rot(("wa", gx, gf), [P, GROUP * PACK], BF16, 3)
-                mx_tiles(("wa", gx, gf), GROUP)
-            o = T[("wa", gx, gf)][:].rearrange("p (t m j) -> p t m j", t=PACK, j=PACK)[:, 2 * h : 2 * h + 2]
-            i = T[("w", gx, gf)][:].rearrange("p j (m t) -> p t m j", t=PACK)[:, 2 * h : 2 * h + 2]
+            o = T[("wa", gx, gf)][:].rearrange("p (t a b j) -> p a t b j", t=PACK, b=2, j=PACK)[:, 32 * h : 32 * h + 32]
+            i = T[("w", gx, gf)][:].rearrange("p j (a b t) -> p a t b j", b=2, t=PACK)[:, 32 * h : 32 * h + 32]
+            if eng == "g":
+                o = T[("wa", gx, gf)][:].rearrange("p (t m j) -> p m j t", t=PACK, j=PACK)[:, 64 * h : 64 * h + 64]
+                i = T[("w", gx, gf)][:].rearrange("p j (m t) -> p m j t", t=PACK)[:, 64 * h : 64 * h + 64]
             lay(o, i, eng)
 
-        def wa_q(gx, gf, h):
-            quantize(("wa", gx, gf), T[("wa", gx, gf)][:, 1024 * h : 1024 * (h + 1)], 256 * h, 256 * (h + 1))
+        def wa_q(gx, gf):
+            mx_tiles(("wa", gx, gf), GROUP)
+            quantize(("wa", gx, gf), T[("wa", gx, gf)][:], 0, GROUP)
+
+        def heat_setup():
+            ones = kept(("ones",), [P, GROUP], BF16)
+            nc.vector.memset(ones[:], 1.0)
+            mx_tiles(("ones",), P)
+            quantize(("ones",), ones[:], 0, P)
+
+        def heat(k):
+            bk = bank(("heat", k), "mm")
+            for j in range(4):
+                nc.tensor.matmul_mx(
+                    out=bk[:, j * P : (j + 1) * P],
+                    lhsT=T[("q", "ones")][:].bitcast(FP8X4), lhsT_scale=T[("s", "ones")][:],
+                    rhs=T[("q", "ones")][:].bitcast(FP8X4), rhs_scale=T[("s", "ones")][:],
+                    start=True, stop=True,
+                )
 
         def wb_turn(gx, gf, h):
             bk = bank(("wt", gx, gf, h), "tr")
@@ -152,16 +171,15 @@ def tile_porthamiltoniannetfield_x1_kernel(tc, z, ctrl, c, w1, g, b1, damp, out_
                 rot(("th", gb, gf), [P, PACK, GROUP], F32, 2)
             nc.scalar.activation(
                 out=T[("th", gb, gf)][:, t, :], in_=T[("m", gb, gf, t)][:], func=ACT.Tanh,
-                bias=T[("b32",)][:, gf, t : t + 1], scale=T[("g32",)][:, gf, t : t + 1],
+                bias=T[("b4",)][:, gf, t : t + 1], scale=T[("g32",)][:, gf, t : t + 1],
             )
 
-        def d_mul(gb, gf, h):
-            if ("dg", gb, gf) not in T:
-                rot(("dg", gb, gf), [P, GROUP * PACK], BF16, 2)
+        def d_mul(gb, gf):
+            t = rot(("dg", gb, gf), [P, GROUP * PACK], BF16, 2)
             nc.vector.tensor_tensor(
-                out=T[("dg", gb, gf)][:, 1024 * h : 1024 * (h + 1)].rearrange("p (c i t) -> p c t i", i=4, t=PACK),
-                in0=T[("th", gb, gf)][:, :, 256 * h : 256 * (h + 1)].rearrange("p t (c i) -> p c t i", i=4),
-                in1=T[("g32",)][:, gf, :].unsqueeze(1).unsqueeze(3).to_broadcast([P, 64, PACK, 4]),
+                out=t[:].rearrange("p (c i t) -> p c t i", i=4, t=PACK),
+                in0=T[("th", gb, gf)][:].rearrange("p t (c i) -> p c t i", i=4),
+                in1=T[("g32",)][:, gf, :].unsqueeze(1).unsqueeze(3).to_broadcast([P, P, PACK, 4]),
                 op=ALU.mult,
             )
 
@@ -181,15 +199,15 @@ def tile_porthamiltoniannetfield_x1_kernel(tc, z, ctrl, c, w1, g, b1, damp, out_
         def s2_v(gb, i, eng):
             v = rot(("v", gb, i), [P, GROUP], F32, 3)
             if eng == "s":
-                nc.scalar.activation(out=v[:], in_=T[("r", gb, 1, i)][:], func=ACT.Copy, scale=ndc[:, i : i + 1])
+                nc.scalar.activation(out=v[:], in_=T[("r", gb, 1, i)][:], func=ACT.Copy, scale=dc[:, i : i + 1])
             elif eng == "v":
-                nc.vector.tensor_scalar(out=v[:], in0=T[("hp", gb, i)][:], scalar1=nd[:, i : i + 1], scalar2=None, op0=ALU.mult)
+                nc.vector.tensor_scalar(out=v[:], in0=T[("hp", gb, i)][:], scalar1=cn[:, 8 + i : 9 + i], scalar2=None, op0=ALU.mult)
             else:
-                nc.gpsimd.tensor_scalar(out=v[:], in0=T[("hp", gb, i)][:], scalar1=nd[:, i : i + 1], scalar2=0.0, op0=ALU.mult, op1=ALU.add)
+                nc.gpsimd.tensor_scalar(out=v[:], in0=T[("hp", gb, i)][:], scalar1=cn[:, 8 + i : 9 + i], scalar2=0.0, op0=ALU.mult, op1=ALU.add)
 
         def s2_stt(gb, i):
             w = rot(("wv", gb, i), [P, GROUP], F32, 3)
-            nc.vector.scalar_tensor_tensor(out=w[:], in0=T[("r", gb, 0, i)][:], scalar=ncl[:, i : i + 1], in1=T[("v", gb, i)][:], op0=ALU.mult, op1=ALU.add)
+            nc.vector.scalar_tensor_tensor(out=w[:], in0=T[("r", gb, 0, i)][:], scalar=cn[:, i : i + 1], in1=T[("v", gb, i)][:], op0=ALU.mult, op1=ALU.add)
 
         def s2_turn(key, gb, i):
             bk = bank(("t" + key, gb, i), "tr")
@@ -202,9 +220,9 @@ def tile_porthamiltoniannetfield_x1_kernel(tc, z, ctrl, c, w1, g, b1, damp, out_
         def s2_dp(gb, i):
             nc.vector.tensor_tensor(
                 out=T[("y", gb)][:, :, N + i * P : N + (i + 1) * P],
-                in0=T[("twv", gb, i)][:].rearrange("p (t n) -> p t n", t=PACK),
-                in1=T[("ctrl", gb)][:, :, i * P : (i + 1) * P],
-                op=ALU.add,
+                in0=T[("ctrl", gb)][:, :, i * P : (i + 1) * P],
+                in1=T[("twv", gb, i)][:].rearrange("p (t n) -> p t n", t=PACK),
+                op=ALU.subtract,
             )
 
         def y_lay(gb, n0, n1, eng):
@@ -233,14 +251,11 @@ def tile_porthamiltoniannetfield_x1_kernel(tc, z, ctrl, c, w1, g, b1, damp, out_
         warm = kept(("warm",), [P, 8], F32)
         ident = kept(("ident",), [P, P], F32)
         rows = kept(("rows",), [P, P], BF16)
-        rows32 = kept(("rows32",), [P, P], F32)
+        ident16 = kept(("ident16",), [P, P], BF16)
         cn = kept(("cn",), [P, 12], F32)
-        ncl = kept(("ncl",), [P, 4], F32)
-        ndc = kept(("ndc",), [P, 4], F32)
+        dc = kept(("dc",), [P, 4], F32)
         kept(("g32",), [P, 2, PACK], F32)
-        kept(("b32",), [P, 2, PACK], F32)
 
-        nd = kept(("nd",), [P, 4], F32)
         for gb in range(2):
             kept(("y", gb), [P, PACK, X], F32)
             kept(("yb", gb), [P, X * PACK], BF16)
@@ -250,10 +265,17 @@ def tile_porthamiltoniannetfield_x1_kernel(tc, z, ctrl, c, w1, g, b1, damp, out_
             load_vec("c4", c)
             load_vec("g4", g)
             load_vec("b4", b1)
+
+        def setup2():
             nc.vector.memset(warm[:], 0.0)
             nc.scalar.activation(out=warm[:, 4:5], in_=warm[:, 0:1], func=ACT.Tanh)
+
+        def setup3():
             make_identity(nc, ident[:])
+
+        def setup4():
             nc.gpsimd.memset(rows[:], 0.0)
+            make_identity(nc, ident16[:])
 
         def load_rows():
             nc.sync.dma_start(out=rows[0:8, :], in_=c.rearrange("(i p) -> i p", p=P))
@@ -261,260 +283,236 @@ def tile_porthamiltoniannetfield_x1_kernel(tc, z, ctrl, c, w1, g, b1, damp, out_
 
         def consts_a():
             nc.vector.tensor_copy(out=T[("g32",)][:], in_=T[("g4",)][:])
-            nc.vector.tensor_copy(out=T[("b32",)][:], in_=T[("b4",)][:])
-
-        def consts_b0():
-            nc.scalar.copy(out=rows32[:], in_=rows[:])
 
         def consts_b():
             bk = bank(("rowt",), "tr")
-            nc.tensor.transpose(bk[:, 0:P], rows32[:], ident[:])
+            nc.tensor.transpose(bk[:].bitcast(BF16)[:, 0:P], rows[:], ident16[:])
 
         def consts_c():
-            nc.vector.tensor_copy(out=cn[:], in_=T[("rowt",)][:, 0:12])
+            nc.scalar.copy(out=cn[:], in_=T[("rowt",)][:].bitcast(BF16)[:, 0:12])
 
         def consts_d():
-            nc.vector.tensor_scalar(out=ncl[:], in0=cn[:, 0:4], scalar1=-1.0, scalar2=None, op0=ALU.mult)
-            nc.vector.tensor_scalar(out=nd[:], in0=cn[:, 8:12], scalar1=-1.0, scalar2=None, op0=ALU.mult)
-            nc.vector.scalar_tensor_tensor(out=ndc[:], in0=cn[:, 4:8], scalar=-1.0, in1=cn[:, 8:12], op0=ALU.mult, op1=ALU.mult)
+            nc.vector.tensor_tensor(out=dc[:], in0=cn[:, 4:8], in1=cn[:, 8:12], op=ALU.mult)
 
         load_w(0, 0)
-        setup()
-        wa_lay(0, 0, 0, "v")
-        consts_a()
-        wb_turn(0, 0, 0)
-        load_z(0, 1, 2, 4)
-        z_turn(0, 1, 1)
-        load_w(0, 1)
-        wa_q(0, 0, 0)
+        load_z(0, 0)
+        load_z(0, 1)
         load_w(1, 0)
+        setup()
+        heat_setup()
+        setup2()
+        setup3()
+        load_z(1, 0)
+        load_w(0, 1)
+        heat(4)
+        setup4()
+        heat(0)
+        heat(1)
+        heat(2)
+        load_z(1, 1)
         wb_turn(0, 0, 1)
-        wa_lay(0, 0, 1, "s")
-        wb_out(0, 0, 0)
-        wa_lay(0, 1, 0, "s")
-        wb_turn(0, 1, 1)
-        load_z(0, 0, 2, 4)
-        load_z(0, 0, 0, 2)
-        load_z(0, 1, 0, 2)
-        z_turn(0, 0, 1)
-        wa_q(0, 0, 1)
         load_w(1, 1)
-        load_z(1, 0, 0, 4)
-        wa_lay(0, 1, 1, "v")
-        x_mul(0, 1, 1)
-        wb_out(0, 0, 1)
-        wa_lay(1, 0, 1, "v")
-        wa_q(0, 1, 1)
-        z_turn(0, 1, 0)
-        wb_out(0, 1, 1)
-        wa_lay(1, 0, 0, "s")
-        z_turn(0, 0, 0)
-        wa_q(1, 0, 1)
-        wa_q(0, 1, 0)
-        wb_q(0, 0)
-        wa_lay(1, 1, 1, "s")
-        wb_turn(0, 1, 0)
-        x_mul(0, 0, 1)
-        load_z(1, 1, 0, 4)
-        wb_turn(1, 1, 0)
-        x_mul(0, 1, 0)
-        wb_out(0, 1, 0)
-        load_rows()
-        wb_out(1, 1, 0)
-        x_mul(0, 0, 0)
-        wa_q(1, 0, 0)
-        x_q(0, 0)
-        x_q(0, 1)
-        z_turn(1, 0, 0)
-        wa_lay(1, 1, 0, "s")
-        z_turn(1, 0, 1)
-        z_turn(1, 1, 0)
-        z_turn(1, 1, 1)
-        s1_mm(0, 0, 1)
-        wb_q(0, 1)
-        s1_tanh(0, 0, 1)
-        s1_mm(0, 0, 3)
         load_ctrl(1)
-        s1_mm(0, 0, 0)
-        s1_tanh(0, 0, 3)
-        x_mul(1, 1, 0)
-        wa_q(1, 1, 0)
-        s1_mm(0, 0, 2)
-        x_mul(1, 1, 1)
-        s1_tanh(0, 0, 0)
-        wa_q(1, 1, 1)
-        s1_tanh(0, 0, 2)
-        s1_mm(0, 1, 1)
-        s1_mm(0, 1, 3)
-        x_mul(1, 0, 1)
-        x_mul(1, 0, 0)
-        s1_mm(0, 1, 0)
-        s1_mm(0, 1, 2)
-        x_q(1, 1)
-        consts_b0()
-        wb_turn(1, 1, 1)
-        x_q(1, 0)
-        d_mul(0, 0, 1)
-        s1_tanh(0, 1, 1)
-        wb_turn(1, 0, 0)
+        wa_lay(0, 0, 1, "v")
+        load_rows()
+        wa_lay(0, 0, 0, "v")
+        wb_turn(0, 0, 0)
+        wb_out(0, 0, 1)
+        consts_a()
+        heat(3)
+        wa_q(0, 0)
+        z_turn(0, 1, 0)
+        wb_out(0, 0, 0)
+        z_turn(0, 0, 1)
+        z_turn(0, 0, 0)
+        wb_q(0, 0)
+        x_mul(0, 1, 0)
+        wa_lay(1, 0, 0, "s")
+        load_ctrl(0)
+        z_turn(0, 1, 1)
+        x_mul(0, 0, 1)
         wb_turn(1, 0, 1)
-        consts_b()
-        s1_tanh(0, 1, 3)
-        s1_mm(1, 0, 1)
-        s1_tanh(0, 1, 0)
-        s1_tanh(0, 1, 2)
-        wb_out(1, 1, 1)
-        d_mul(0, 0, 0)
-        d_mul(0, 1, 0)
-        s1_mm(1, 0, 3)
-        wb_out(1, 0, 0)
+        wa_lay(1, 0, 1, "s")
+        x_mul(0, 0, 0)
+        z_turn(1, 0, 0)
+        x_mul(0, 1, 1)
+        x_q(0, 0)
+        z_turn(1, 1, 0)
+        x_q(0, 1)
+        wa_lay(0, 1, 0, "s")
+        wa_q(1, 0)
+        s1_mm(0, 0, 3)
+        wa_lay(0, 1, 1, "v")
         wb_out(1, 0, 1)
-        d_mul(0, 1, 1)
+        x_mul(1, 0, 0)
+        z_turn(1, 0, 1)
+        s1_tanh(0, 0, 3)
+        wa_q(0, 1)
+        wa_lay(1, 1, 0, "s")
+        z_turn(1, 1, 1)
+        wb_turn(0, 1, 1)
+        x_mul(1, 1, 0)
+        s1_mm(0, 0, 0)
+        wb_out(0, 1, 1)
+        wa_lay(1, 1, 1, "v")
+        x_mul(1, 0, 1)
+        s1_mm(0, 0, 1)
+        wa_q(1, 1)
+        s1_tanh(0, 0, 0)
+        x_mul(1, 1, 1)
+        s1_mm(0, 0, 2)
+        s1_mm(0, 1, 3)
+        s1_mm(0, 1, 2)
+        s1_tanh(0, 0, 1)
+        x_q(1, 0)
+        s1_tanh(0, 0, 2)
+        s1_tanh(0, 1, 3)
+        x_q(1, 1)
+        wb_turn(0, 1, 0)
+        s1_tanh(0, 1, 2)
+        wb_turn(1, 0, 0)
+        d_mul(0, 0)
+        wb_out(0, 1, 0)
+        wb_out(1, 0, 0)
+        s1_mm(0, 1, 1)
+        s1_mm(0, 1, 0)
+        s1_tanh(0, 1, 1)
         wb_q(1, 0)
-        s1_tanh(1, 0, 1)
+        wb_turn(1, 1, 1)
+        s1_tanh(0, 1, 0)
+        d_q(0, 0)
+        consts_b()
+        wb_turn(1, 1, 0)
         consts_c()
+        d_mul(0, 1)
+        wb_out(1, 1, 1)
+        s1_mm(1, 0, 0)
+        wb_out(1, 1, 0)
+        s1_mm(1, 0, 2)
+        s1_tanh(1, 0, 0)
+        s1_tanh(1, 0, 2)
+        s1_mm(1, 0, 1)
+        s1_mm(1, 0, 3)
+        s1_tanh(1, 0, 1)
+        s1_mm(1, 1, 0)
+        wb_q(1, 1)
+        consts_d()
         d_q(0, 1)
         s1_tanh(1, 0, 3)
-        s1_mm(1, 0, 2)
-        s1_mm(1, 1, 0)
-        s1_mm(1, 1, 3)
-        s1_tanh(1, 0, 2)
-        d_q(0, 0)
-        s1_mm(1, 0, 0)
-        consts_d()
-        s1_mm(1, 1, 2)
-        s1_tanh(1, 1, 0)
-        s1_tanh(1, 1, 3)
-        wb_q(1, 1)
-        s1_tanh(1, 0, 0)
         s1_mm(1, 1, 1)
-        d_mul(1, 0, 1)
-        s1_tanh(1, 1, 2)
-        s2_mm(0, 1, 1)
-        s2_mm(0, 1, 0)
-        d_mul(1, 0, 0)
+        wb_q(0, 1)
+        s1_tanh(1, 1, 0)
+        s1_mm(1, 1, 3)
+        d_mul(1, 0)
         s1_tanh(1, 1, 1)
-        s2_mm(0, 1, 3)
-        s2_mm(0, 0, 1)
-        s2_hp(0, 1)
-        s2_hp(0, 0)
-        s2_v(0, 1, "s")
-        s2_turn("hp", 0, 1)
-        d_mul(1, 1, 1)
-        s2_stt(0, 1)
-        d_mul(1, 1, 0)
-        s2_hp(0, 3)
-        s2_turn("hp", 0, 0)
-        s2_v(0, 0, "s")
-        s2_v(0, 3, "v")
-        s2_dq(0, 1, "s")
+        s1_mm(1, 1, 2)
+        s1_tanh(1, 1, 3)
+        s2_mm(0, 1, 0)
+        s1_tanh(1, 1, 2)
         s2_mm(0, 1, 2)
-        s2_hp(0, 2)
-        s2_turn("hp", 0, 3)
-        y_lay(0, 128, 256, "s")
-        d_q(1, 0)
-        s2_turn("wv", 0, 1)
+        s2_hp(0, 0)
+        d_mul(1, 1)
         s2_mm(0, 0, 0)
-        s2_dq(0, 3, "s")
+        s2_hp(0, 2)
+        s2_mm(0, 1, 3)
+        s2_v(0, 0, "s")
+        s2_turn("hp", 0, 0)
         s2_v(0, 2, "s")
-        d_q(1, 1)
-        s2_dq(0, 0, "s")
-        load_ctrl(0)
-        s2_dp(0, 1)
         s2_turn("hp", 0, 2)
+        s2_mm(0, 1, 1)
         s2_stt(0, 0)
         s2_mm(0, 0, 2)
-        s2_mm(1, 1, 3)
+        d_q(1, 1)
+        s2_dq(0, 0, "s")
         s2_mm(0, 0, 3)
-        y_lay(0, 0, 128, "v")
+        s2_hp(0, 3)
+        s2_hp(0, 1)
         s2_turn("wv", 0, 0)
-        s2_mm(1, 0, 3)
-        s2_hp(1, 3)
+        s2_v(0, 3, "v")
+        s2_turn("hp", 0, 3)
         s2_stt(0, 2)
-        s2_v(1, 3, "v")
-        s2_mm(1, 1, 0)
-        s2_dp(0, 0)
-        s2_stt(0, 3)
-        s2_stt(1, 3)
-        y_lay(0, 640, 768, "s")
         s2_dq(0, 2, "s")
-        y_q(0, 0, 256)
-        y_lay(0, 384, 512, "s")
+        s2_turn("hp", 0, 1)
+        s2_stt(0, 3)
+        s2_v(0, 1, "s")
         s2_turn("wv", 0, 2)
-        s2_hp(1, 0)
+        d_q(1, 0)
+        s2_dq(0, 3, "s")
+        s2_mm(0, 0, 1)
+        s2_dp(0, 0)
+        s2_dq(0, 1, "s")
+        s2_stt(0, 1)
+        s2_mm(1, 1, 3)
+        y_lay(0, 256, 512, "s")
+        y_store(0, 0, 512)
         s2_turn("wv", 0, 3)
-        y_store(0, 256, 512)
-        y_lay(0, 256, 384, "v")
-        s2_mm(1, 1, 2)
-        y_store(0, 512, 768)
-        s2_v(1, 0, "s")
-        s2_dp(0, 3)
         s2_dp(0, 2)
-        y_q(0, 256, 512)
-        y_lay(0, 768, 896, "v")
-        y_lay(0, 512, 640, "s")
-        s2_hp(1, 2)
+        s2_turn("wv", 0, 1)
+        s2_mm(1, 0, 3)
+        s2_dp(0, 3)
+        s2_hp(1, 3)
+        s2_dp(0, 1)
         s2_mm(1, 1, 1)
-        y_lay(0, 896, 1024, "s")
-        s2_mm(1, 0, 1)
-        s2_v(1, 2, "v")
-        s2_turn("hp", 1, 3)
-        s2_turn("hp", 1, 2)
-        y_q(0, 768, 1024)
-        y_q(0, 512, 768)
-        s2_dq(1, 3, "s")
+        s2_v(1, 3, "s")
+        y_lay(0, 0, 256, "v")
+        y_lay(0, 768, 1024, "s")
+        s2_mm(1, 1, 2)
+        y_store(0, 512, 1024)
         s2_hp(1, 1)
-        y_store(0, 0, 256)
-        s2_mm(1, 0, 2)
-        s2_dq(1, 2, "v")
-        y_store(0, 768, 1024)
-        y_store(1, 384, 512)
-        y_lay(1, 384, 512, "s")
-        s_store(0, 1, "y")
+        s2_mm(1, 1, 0)
+        s2_stt(1, 3)
+        y_lay(0, 512, 768, "v")
+        y_q(0, 0, 512)
         s2_turn("wv", 1, 3)
-        s2_stt(1, 2)
-        s2_mm(1, 0, 0)
-        s2_turn("hp", 1, 0)
+        s2_turn("hp", 1, 3)
+        s2_hp(1, 0)
+        s2_turn("hp", 1, 1)
         s2_dp(1, 3)
-        y_lay(1, 256, 384, "s")
-        s2_turn("wv", 1, 2)
-        s2_v(1, 1, "s")
-        s_store(0, 2, "y")
-        s_store(0, 3, "y")
+        s2_hp(1, 2)
+        s2_turn("hp", 1, 0)
+        y_store(1, 896, 1024)
+        s2_dq(1, 1, "s")
+        y_q(0, 512, 1024)
+        s2_turn("hp", 1, 2)
+        s2_v(1, 2, "v")
+        s2_dq(1, 3, "s")
+        s_store(0, 0, "y")
+        s2_mm(1, 0, 2)
+        s2_v(1, 1, "v")
         q_store(0, 0, 1024)
+        s2_dq(1, 2, "v")
+        s_store(0, 3, "y")
+        s_store(0, 1, "y")
+        s_store(0, 2, "y")
+        s2_mm(1, 0, 1)
+        s2_dq(1, 0, "s")
+        s2_stt(1, 2)
+        s2_v(1, 0, "s")
+        s2_mm(1, 0, 0)
+        s2_turn("wv", 1, 2)
+        y_store(1, 0, 512)
+        s2_stt(1, 1)
+        s2_turn("wv", 1, 1)
         s2_stt(1, 0)
         s2_dp(1, 2)
-        s2_stt(1, 1)
-        y_store(1, 896, 1024)
-        s2_dq(1, 0, "s")
-        y_store(1, 256, 384)
-        y_q(1, 384, 512)
-        s2_turn("hp", 1, 1)
         s2_turn("wv", 1, 0)
-        s2_turn("wv", 1, 1)
-        y_q(1, 256, 384)
-        s2_dq(1, 1, "s")
-        s_store(0, 0, "y")
-        s2_dp(1, 0)
-        y_store(1, 768, 896)
         s2_dp(1, 1)
-        y_lay(1, 768, 896, "s")
-        y_lay(1, 896, 1024, "v")
-        y_lay(1, 640, 768, "v")
-        y_lay(1, 0, 128, "s")
-        y_q(1, 768, 896)
-        y_store(1, 0, 256)
-        y_q(1, 896, 1024)
-        y_lay(1, 512, 640, "s")
-        q_store(1, 256, 512)
-        y_lay(1, 128, 256, "s")
+        y_lay(1, 256, 512, "s")
+        y_lay(1, 0, 256, "s")
+        y_store(1, 768, 896)
+        s2_dp(1, 0)
+        y_lay(1, 512, 768, "s")
         y_store(1, 512, 768)
-        q_store(1, 768, 1024)
+        y_lay(1, 768, 896, "v")
+        y_lay(1, 896, 1024, "v")
+        y_q(1, 0, 512)
+        q_store(1, 0, 512)
+        y_q(1, 896, 1024)
+        y_q(1, 768, 896)
         y_q(1, 512, 768)
-        y_q(1, 0, 256)
-        q_store(1, 512, 768)
+        s_store(1, 3, "s")
+        q_store(1, 896, 1024)
         s_store(1, 2, "s")
         s_store(1, 0, "y")
+        q_store(1, 512, 896)
         s_store(1, 1, "y")
-        s_store(1, 3, "s")
-        q_store(1, 0, 256)

@@ -17,6 +17,10 @@ N = X // 2
 P = 128
 PACK = 4
 GROUP = P * PACK
+GROUPS = X // GROUP
+BLOCKS = N // P
+WORDS = GROUP // 2
+LO, HI = 0, 1
 FLOPS = 4 * B * X * F
 
 
@@ -28,491 +32,487 @@ def tile_porthamiltoniannetfield_x1_kernel(tc, z, ctrl, c, w1, g, b1, damp, out_
         psum = ctx.enter_context(tc.psum_pool(name="psum", bufs=4))
         ctx.enter_context(tc.manual_schedule())
 
-        T = {}
+        tiles = {}
+
+        def label(key):
+            return "_".join([str(part) for part in key])
 
         def kept(key, shape, dtype):
-            name = "_".join([str(k) for k in key])
-            T[key] = keep.tile(shape, dtype, name=name, align_bytes=64)
-            return T[key]
+            tiles[key] = keep.tile(shape, dtype, name=label(key), align_bytes=64)
+            return tiles[key]
 
-        def rot(key, shape, dtype, bufs):
-            name = "_".join([str(k) for k in key])
-            T[key] = work.tile(shape, dtype, name=name, tag=key[0], bufs=bufs, align_bytes=64)
-            return T[key]
+        def staged(key, shape, dtype, bufs):
+            if key not in tiles:
+                tiles[key] = work.tile(shape, dtype, name=label(key), tag=key[0], bufs=bufs, align_bytes=64)
+            return tiles[key]
 
         def bank(key, tag):
-            name = "_".join([str(k) for k in key])
-            T[key] = psum.tile([P, GROUP], F32, name=name, tag=tag)
-            return T[key]
+            tiles[key] = psum.tile([P, GROUP], F32, name=label(key), tag=tag)
+            return tiles[key]
 
-        def load_z(gb, h):
-            if ("z", gb) not in T:
-                kept(("z", gb), [P, PACK, X], BF16)
-            src = z[GROUP * gb : GROUP * (gb + 1), :].rearrange("(p t) x -> p t x", t=PACK)
-            nc.sync.dma_start(out=T[("z", gb)][:, 2 * h : 2 * h + 2, :], in_=src[:, 2 * h : 2 * h + 2, :])
+        def group(index):
+            return slice(GROUP * index, GROUP * (index + 1))
 
-        def load_w(gx, gf):
-            t = kept(("w", gx, gf), [P, PACK, GROUP], BF16)
-            nc.sync.dma_start(out=t[:], in_=w1[GROUP * gx : GROUP * (gx + 1), GROUP * gf : GROUP * (gf + 1)].rearrange("(p j) f -> p j f", j=PACK))
+        def block(index):
+            return slice(P * index, P * (index + 1))
 
-        def load_ctrl(gb):
-            t = kept(("ctrl", gb), [P, PACK, N], BF16)
-            nc.sync.dma_start(out=t[:], in_=ctrl[GROUP * gb : GROUP * (gb + 1), :].rearrange("(p t) n -> p t n", t=PACK))
+        def quantize(key, width):
+            codes = kept(("codes",) + key, [P, width], U32)
+            scales = kept(("scales",) + key, [P, width], U8)
+            nc.vector.quantize_mx(out=codes[:].bitcast(FP8X4), scales=scales[:], in_=tiles[key][:])
 
-        def load_vec(name, vec):
-            t = kept((name,), [P, 2, PACK], BF16)
-            nc.scalar.dma_start(out=t[:], in_=vec.rearrange("(g p t) -> p g t", g=2, t=PACK))
-
-        def mx_tiles(key, width):
-            kept(("q",) + key, [P, width], U32)
-            kept(("s",) + key, [P, width], U8)
-
-        def quantize(key, src, lo, hi):
-            nc.vector.quantize_mx(out=T[("q",) + key][:, lo:hi].bitcast(FP8X4), scales=T[("s",) + key][:, lo:hi], in_=src)
-
-        def mx_pass(out, lkey, l0, rkey, first):
+        def mx_pass(out, lhs_key, lhs_cols, rhs_key, start, stop):
             nc.tensor.matmul_mx(
                 out=out,
-                lhsT=T[("q",) + lkey][:, l0 : l0 + P].bitcast(FP8X4),
-                lhsT_scale=T[("s",) + lkey][:, l0 : l0 + P],
-                rhs=T[("q",) + rkey][:].bitcast(FP8X4),
-                rhs_scale=T[("s",) + rkey][:],
-                start=first,
-                stop=not first,
+                lhsT=tiles[("codes",) + lhs_key][:, lhs_cols].bitcast(FP8X4),
+                lhsT_scale=tiles[("scales",) + lhs_key][:, lhs_cols],
+                rhs=tiles[("codes",) + rhs_key][:].bitcast(FP8X4),
+                rhs_scale=tiles[("scales",) + rhs_key][:],
+                start=start,
+                stop=stop,
             )
 
-        def lay(o, i, eng):
-            if eng == "v":
-                nc.vector.tensor_copy(out=o, in_=i)
-            elif eng == "s":
-                nc.scalar.copy(out=o, in_=i)
+        def copy_on(engine, out, in_):
+            if engine == "vector":
+                nc.vector.tensor_copy(out=out, in_=in_)
             else:
-                nc.gpsimd.tensor_scalar(out=o, in0=i, scalar1=1.0, scalar2=0.0, op0=ALU.mult, op1=ALU.add)
+                nc.scalar.copy(out=out, in_=in_)
+
+        def load_z(gb, h):
+            if h == 0:
+                kept(("z", gb), [P, PACK, X], BF16)
+            rows = z[group(gb), :].rearrange("(p t) x -> p t x", t=PACK)
+            nc.sync.dma_start(out=tiles[("z", gb)][:, 2 * h : 2 * h + 2, :], in_=rows[:, 2 * h : 2 * h + 2, :])
+
+        def load_w(gx, gf):
+            w = kept(("w", gx, gf), [P, PACK, GROUP], BF16)
+            nc.sync.dma_start(out=w[:], in_=w1[group(gx), group(gf)].rearrange("(p j) f -> p j f", j=PACK))
+
+        def load_ctrl(gb):
+            u = kept(("ctrl", gb), [P, PACK, N], BF16)
+            nc.sync.dma_start(out=u[:], in_=ctrl[group(gb), :].rearrange("(p t) n -> p t n", t=PACK))
+
+        def load_slots(name, vec):
+            slots = kept((name,), [P, GROUPS, PACK], BF16)
+            nc.scalar.dma_start(out=slots[:], in_=vec.rearrange("(a p t) -> p a t", a=GROUPS, t=PACK))
+            return slots
 
         def z_turn(gb, gx, h):
-            bk = bank(("zt", gb, gx, h), "tr")
-            words = T[("z", gb)][:].rearrange("p t x -> p (t x)").bitcast(F32)
+            turned = bank(("zt", gb, gx, h), "turn")
+            words = tiles[("z", gb)][:].rearrange("p t x -> p (t x)").bitcast(F32)
             for u in range(2):
                 for tt in range(2):
-                    w0 = (2 * h + tt) * 512 + gx * 256
-                    nc.tensor.transpose(bk[:, (2 * u + tt) * P : (2 * u + tt + 1) * P], words[:, w0 + u : w0 + 256 : 2], ident[:])
+                    first = ((2 * h + tt) * GROUPS + gx) * WORDS
+                    nc.tensor.transpose(turned[:, block(2 * u + tt)], words[:, first + u : first + WORDS : 2], ident[:])
 
         def x_mul(gb, gx, h):
-            if ("xg", gb, gx) not in T:
-                rot(("xg", gb, gx), [P, GROUP * PACK], BF16, 2)
+            x = staged(("x", gb, gx), [P, GROUP * PACK], BF16, 2)
+            half = GROUP * PACK // 2
             nc.vector.tensor_tensor(
-                out=T[("xg", gb, gx)][:, 1024 * h : 1024 * (h + 1)].rearrange("p (r u e) -> p r u e", u=2, e=2),
-                in0=T[("zt", gb, gx, h)][:].bitcast(BF16).rearrange("p (u r e) -> p r u e", u=2, e=2),
-                in1=T[("c4",)][:, gx, :].rearrange("p (u e) -> p u e", e=2).unsqueeze(1).to_broadcast([P, 256, 2, 2]),
+                out=x[:, half * h : half * (h + 1)].rearrange("p (r u e) -> p r u e", u=2, e=2),
+                in0=tiles[("zt", gb, gx, h)][:].bitcast(BF16).rearrange("p (u r e) -> p r u e", u=2, e=2),
+                in1=c_slots[:, gx, :].rearrange("p (u e) -> p u e", e=2).unsqueeze(1).to_broadcast([P, 2 * P, 2, 2]),
                 op=ALU.mult,
             )
 
-        def x_q(gb, gx):
-            mx_tiles(("x", gb, gx), GROUP)
-            quantize(("x", gb, gx), T[("xg", gb, gx)][:], 0, GROUP)
+        def x_quant(gb, gx):
+            quantize(("x", gb, gx), GROUP)
 
-        def wa_lay(gx, gf, h, eng):
-            if ("wa", gx, gf) not in T:
-                rot(("wa", gx, gf), [P, GROUP * PACK], BF16, 3)
-            o = T[("wa", gx, gf)][:].rearrange("p (t a b j) -> p a t b j", t=PACK, b=2, j=PACK)[:, 32 * h : 32 * h + 32]
-            i = T[("w", gx, gf)][:].rearrange("p j (a b t) -> p a t b j", b=2, t=PACK)[:, 32 * h : 32 * h + 32]
-            if eng == "g":
-                o = T[("wa", gx, gf)][:].rearrange("p (t m j) -> p m j t", t=PACK, j=PACK)[:, 64 * h : 64 * h + 64]
-                i = T[("w", gx, gf)][:].rearrange("p j (m t) -> p m j t", t=PACK)[:, 64 * h : 64 * h + 64]
-            lay(o, i, eng)
+        def wa_lay(gx, gf, h, engine):
+            wa = staged(("wa", gx, gf), [P, GROUP * PACK], BF16, 3)
+            pairs = slice(P // 4 * h, P // 4 * (h + 1))
+            copy_on(
+                engine,
+                wa[:].rearrange("p (t a b j) -> p a t b j", t=PACK, b=2, j=PACK)[:, pairs],
+                tiles[("w", gx, gf)][:].rearrange("p j (a b t) -> p a t b j", b=2, t=PACK)[:, pairs],
+            )
 
-        def wa_q(gx, gf):
-            mx_tiles(("wa", gx, gf), GROUP)
-            quantize(("wa", gx, gf), T[("wa", gx, gf)][:], 0, GROUP)
-
-        def heat_setup():
-            ones = kept(("ones",), [P, GROUP], BF16)
-            nc.vector.memset(ones[:], 1.0)
-            mx_tiles(("ones",), P)
-            quantize(("ones",), ones[:], 0, P)
-
-        def heat(k):
-            bk = bank(("heat", k), "mm")
-            for j in range(4):
-                nc.tensor.matmul_mx(
-                    out=bk[:, j * P : (j + 1) * P],
-                    lhsT=T[("q", "ones")][:].bitcast(FP8X4), lhsT_scale=T[("s", "ones")][:],
-                    rhs=T[("q", "ones")][:].bitcast(FP8X4), rhs_scale=T[("s", "ones")][:],
-                    start=True, stop=True,
-                )
+        def wa_quant(gx, gf):
+            quantize(("wa", gx, gf), GROUP)
 
         def wb_turn(gx, gf, h):
-            bk = bank(("wt", gx, gf, h), "tr")
-            words = T[("w", gx, gf)][:].rearrange("p j f -> p (j f)").bitcast(F32)
+            turned = bank(("wt", gx, gf, h), "turn")
+            words = tiles[("w", gx, gf)][:].rearrange("p j f -> p (j f)").bitcast(F32)
             for jj in range(2):
                 for u in range(2):
-                    w0 = (2 * h + jj) * 256
-                    nc.tensor.transpose(bk[:, (2 * jj + u) * P : (2 * jj + u + 1) * P], words[:, w0 + u : w0 + 256 : 2], ident[:])
+                    first = (2 * h + jj) * WORDS
+                    nc.tensor.transpose(turned[:, block(2 * jj + u)], words[:, first + u : first + WORDS : 2], ident[:])
 
         def wb_out(gx, gf, h):
-            if ("wb", gx, gf) not in T:
-                rot(("wb", gx, gf), [P, GROUP * PACK], BF16, 2)
+            wb = staged(("wb", gx, gf), [P, GROUP * PACK], BF16, 2)
             nc.scalar.copy(
-                out=T[("wb", gx, gf)][:].bitcast(F32).rearrange("p (r h q) -> p r h q", h=2, q=4)[:, :, h, :],
-                in_=T[("wt", gx, gf, h)][:].rearrange("p (q r) -> p r q", q=4),
+                out=wb[:].bitcast(F32).rearrange("p (r h q) -> p r h q", h=2, q=4)[:, :, h, :],
+                in_=tiles[("wt", gx, gf, h)][:].rearrange("p (q r) -> p r q", q=4),
             )
 
-        def wb_q(gx, gf):
-            mx_tiles(("wb", gx, gf), GROUP)
-            quantize(("wb", gx, gf), T[("wb", gx, gf)][:], 0, GROUP)
+        def wb_quant(gx, gf):
+            quantize(("wb", gx, gf), GROUP)
 
-        def s1_mm(gb, gf, t):
-            bk = bank(("m", gb, gf, t), "mm")
-            for gx in range(2):
-                mx_pass(bk[:], ("wa", gx, gf), t * P, ("x", gb, gx), gx == 0)
+        def m_mm(gb, gf, t):
+            m = bank(("m", gb, gf, t), "sum")
+            for gx in range(GROUPS):
+                mx_pass(m[:], ("wa", gx, gf), block(t), ("x", gb, gx), gx == 0, gx == GROUPS - 1)
 
-        def s1_tanh(gb, gf, t):
-            if ("th", gb, gf) not in T:
-                rot(("th", gb, gf), [P, PACK, GROUP], F32, 2)
+        def m_tanh(gb, gf, t):
+            th = staged(("th", gb, gf), [P, PACK, GROUP], F32, 2)
             nc.scalar.activation(
-                out=T[("th", gb, gf)][:, t, :], in_=T[("m", gb, gf, t)][:], func=ACT.Tanh,
-                bias=T[("b4",)][:, gf, t : t + 1], scale=T[("g32",)][:, gf, t : t + 1],
+                out=th[:, t, :],
+                in_=tiles[("m", gb, gf, t)][:],
+                func=ACT.Tanh,
+                bias=b_slots[:, gf, t : t + 1],
+                scale=g32[:, gf, t : t + 1],
             )
 
-        def d_mul(gb, gf):
-            t = rot(("dg", gb, gf), [P, GROUP * PACK], BF16, 2)
+        def delta_mul(gb, gf):
+            delta = staged(("delta", gb, gf), [P, GROUP * PACK], BF16, 2)
             nc.vector.tensor_tensor(
-                out=t[:].rearrange("p (c i t) -> p c t i", i=4, t=PACK),
-                in0=T[("th", gb, gf)][:].rearrange("p t (c i) -> p c t i", i=4),
-                in1=T[("g32",)][:, gf, :].unsqueeze(1).unsqueeze(3).to_broadcast([P, P, PACK, 4]),
+                out=delta[:].rearrange("p (c i t) -> p c t i", i=4, t=PACK),
+                in0=tiles[("th", gb, gf)][:].rearrange("p t (c i) -> p c t i", i=4),
+                in1=g32[:, gf, :].unsqueeze(1).unsqueeze(3).to_broadcast([P, GROUP // 4, PACK, 4]),
                 op=ALU.mult,
             )
 
-        def d_q(gb, gf):
-            mx_tiles(("d", gb, gf), GROUP)
-            quantize(("d", gb, gf), T[("dg", gb, gf)][:], 0, GROUP)
+        def delta_quant(gb, gf):
+            quantize(("delta", gb, gf), GROUP)
 
-        def s2_mm(gb, gx, i):
-            bk = bank(("r", gb, gx, i), "mm")
-            for gf in range(2):
-                mx_pass(bk[:], ("wb", gx, gf), i * P, ("d", gb, gf), gf == 0)
+        def r_mm(gb, gx, i):
+            r = bank(("r", gb, gx, i), "sum")
+            for gf in range(GROUPS):
+                mx_pass(r[:], ("wb", gx, gf), block(i), ("delta", gb, gf), gf == 0, gf == GROUPS - 1)
 
-        def s2_hp(gb, i):
-            hp = rot(("hp", gb, i), [P, GROUP], F32, 3)
-            nc.scalar.activation(out=hp[:], in_=T[("r", gb, 1, i)][:], func=ACT.Copy, scale=cn[:, 4 + i : 5 + i])
+        def hp_out(gb, i):
+            hp = staged(("hp", gb, i), [P, GROUP], F32, BLOCKS)
+            nc.scalar.activation(out=hp[:], in_=tiles[("r", gb, HI, i)][:], func=ACT.Copy, scale=cols[:, BLOCKS + i : BLOCKS + i + 1])
 
-        def s2_v(gb, i, eng):
-            v = rot(("v", gb, i), [P, GROUP], F32, 3)
-            if eng == "s":
-                nc.scalar.activation(out=v[:], in_=T[("r", gb, 1, i)][:], func=ACT.Copy, scale=dc[:, i : i + 1])
-            elif eng == "v":
-                nc.vector.tensor_scalar(out=v[:], in0=T[("hp", gb, i)][:], scalar1=cn[:, 8 + i : 9 + i], scalar2=None, op0=ALU.mult)
+        def damped(gb, i, engine):
+            dh = staged(("dh", gb, i), [P, GROUP], F32, BLOCKS)
+            if engine == "scalar":
+                nc.scalar.activation(out=dh[:], in_=tiles[("r", gb, HI, i)][:], func=ACT.Copy, scale=damp_c[:, i : i + 1])
             else:
-                nc.gpsimd.tensor_scalar(out=v[:], in0=T[("hp", gb, i)][:], scalar1=cn[:, 8 + i : 9 + i], scalar2=0.0, op0=ALU.mult, op1=ALU.add)
+                factor = cols[:, 2 * BLOCKS + i : 2 * BLOCKS + i + 1]
+                nc.gpsimd.tensor_scalar(out=dh[:], in0=tiles[("hp", gb, i)][:], scalar1=factor, scalar2=0.0, op0=ALU.mult, op1=ALU.add)
 
-        def s2_stt(gb, i):
-            w = rot(("wv", gb, i), [P, GROUP], F32, 3)
-            nc.vector.scalar_tensor_tensor(out=w[:], in0=T[("r", gb, 0, i)][:], scalar=cn[:, i : i + 1], in1=T[("v", gb, i)][:], op0=ALU.mult, op1=ALU.add)
+        def force(gb, i):
+            fo = staged(("fo", gb, i), [P, GROUP], F32, BLOCKS)
+            nc.vector.scalar_tensor_tensor(
+                out=fo[:], in0=tiles[("r", gb, LO, i)][:], scalar=cols[:, i : i + 1], in1=tiles[("dh", gb, i)][:], op0=ALU.mult, op1=ALU.add
+            )
 
-        def s2_turn(key, gb, i):
-            bk = bank(("t" + key, gb, i), "tr")
+        def turn_back(name, gb, i):
+            turned = bank((name + "t", gb, i), "turn")
             for t in range(PACK):
-                nc.tensor.transpose(bk[:, t * P : (t + 1) * P], T[(key, gb, i)][:, t * P : (t + 1) * P], ident[:])
+                nc.tensor.transpose(turned[:, block(t)], tiles[(name, gb, i)][:, block(t)], ident[:])
 
-        def s2_dq(gb, i, eng):
-            lay(T[("y", gb)][:, :, i * P : (i + 1) * P], T[("thp", gb, i)][:].rearrange("p (t n) -> p t n", t=PACK), eng)
+        def dq_out(gb, i, engine):
+            copy_on(engine, tiles[("y", gb)][:, :, block(i)], tiles[("hpt", gb, i)][:].rearrange("p (t n) -> p t n", t=PACK))
 
-        def s2_dp(gb, i):
+        def dp_out(gb, i):
             nc.vector.tensor_tensor(
-                out=T[("y", gb)][:, :, N + i * P : N + (i + 1) * P],
-                in0=T[("ctrl", gb)][:, :, i * P : (i + 1) * P],
-                in1=T[("twv", gb, i)][:].rearrange("p (t n) -> p t n", t=PACK),
+                out=tiles[("y", gb)][:, :, block(BLOCKS + i)],
+                in0=tiles[("ctrl", gb)][:, :, block(i)],
+                in1=tiles[("fot", gb, i)][:].rearrange("p (t n) -> p t n", t=PACK),
                 op=ALU.subtract,
             )
 
-        def y_lay(gb, n0, n1, eng):
-            o = T[("yb", gb)][:, PACK * n0 : PACK * n1].rearrange("p (c i t) -> p c t i", i=4, t=PACK)
-            i = T[("y", gb)][:, :, n0:n1].rearrange("p t (c i) -> p c t i", i=4)
-            lay(o, i, eng)
+        def y_lay(gb, first, last, engine):
+            laid = tiles[("y16", gb)][:, GROUP * first : GROUP * last]
+            y = tiles[("y", gb)][:, :, P * first : P * last]
+            if engine == "gpsimd":
+                nc.gpsimd.tensor_scalar(
+                    out=laid.rearrange("p (n t) -> p n t", t=PACK),
+                    in0=y.rearrange("p t n -> p n t"),
+                    scalar1=1.0,
+                    scalar2=0.0,
+                    op0=ALU.mult,
+                    op1=ALU.add,
+                )
+            else:
+                nc.scalar.copy(out=laid.rearrange("p (c i t) -> p c t i", i=4, t=PACK), in_=y.rearrange("p t (c i) -> p c t i", i=4))
 
-        def y_q(gb, n0, n1):
-            quantize(("y", gb), T[("yb", gb)][:, PACK * n0 : PACK * n1], n0, n1)
-
-        def y_store(gb, n0, n1):
-            nc.sync.dma_start(
-                out=out_0[GROUP * gb : GROUP * (gb + 1), n0:n1].rearrange("(p t) n -> p t n", t=PACK), in_=T[("y", gb)][:, :, n0:n1]
+        def y_quant(gb, first, last):
+            nc.vector.quantize_mx(
+                out=tiles[("y_codes", gb)][:, P * first : P * last].bitcast(FP8X4),
+                scales=y_scales[:, gb, P * first : P * last],
+                in_=tiles[("y16", gb)][:, GROUP * first : GROUP * last],
             )
 
-        def q_store(gb, n0, n1):
-            nc.sync.dma_start(
-                out=out_1[gb].rearrange("p m t -> p (m t)").bitcast(I32)[:, n0:n1], in_=T[("q", "y", gb)][:, n0:n1].bitcast(I32)
+        def y_store(gb, first, last):
+            span = slice(P * first, P * last)
+            nc.sync.dma_start(out=out_0[group(gb), span].rearrange("(p t) n -> p t n", t=PACK), in_=tiles[("y", gb)][:, :, span])
+
+        def codes_store(gb, first, last):
+            span = slice(P * first, P * last)
+            words = out_1[gb].rearrange("p m t -> p (m t)").bitcast(I32)
+            nc.sync.dma_start(out=words[:, span], in_=tiles[("y_codes", gb)][:, span].bitcast(I32))
+
+        def scales_store(q, queue):
+            queue.dma_start(
+                out=out_2[:, 4 * q : 4 * q + 4, :].rearrange("a r m -> r a m").bitcast(I32),
+                in_=y_scales[32 * q : 32 * q + 4, :, :].bitcast(I32),
             )
 
-        def s_store(gb, q, eng):
-            (nc.sync if eng == "y" else nc.scalar).dma_start(
-                out=out_2[gb, 4 * q : 4 * q + 4, :].bitcast(I32), in_=T[("s", "y", gb)][32 * q : 32 * q + 4, :].bitcast(I32)
-            )
+        def heat(k):
+            idle = bank(("heat", k), "sum")
+            for j in range(PACK):
+                mx_pass(idle[:, block(j)], ("ones",), block(0), ("ones",), True, True)
 
-        warm = kept(("warm",), [P, 8], F32)
         ident = kept(("ident",), [P, P], F32)
-        rows = kept(("rows",), [P, P], BF16)
         ident16 = kept(("ident16",), [P, P], BF16)
-        cn = kept(("cn",), [P, 12], F32)
-        dc = kept(("dc",), [P, 4], F32)
-        kept(("g32",), [P, 2, PACK], F32)
-
-        for gb in range(2):
+        warm = kept(("warm",), [P, 8], F32)
+        ones = kept(("ones",), [P, GROUP], BF16)
+        g32 = kept(("g32",), [P, GROUPS, PACK], F32)
+        rows = kept(("rows",), [P, P], BF16)
+        cols = kept(("cols",), [P, 3 * BLOCKS], F32)
+        damp_c = kept(("damp_c",), [P, BLOCKS], F32)
+        y_scales = kept(("y_scales",), [P, GROUPS, X], U8)
+        for gb in range(GROUPS):
             kept(("y", gb), [P, PACK, X], F32)
-            kept(("yb", gb), [P, X * PACK], BF16)
-            mx_tiles(("y", gb), X)
+            kept(("y16", gb), [P, X * PACK], BF16)
+            kept(("y_codes", gb), [P, X], U32)
 
-        def setup():
-            load_vec("c4", c)
-            load_vec("g4", g)
-            load_vec("b4", b1)
-
-        def setup2():
-            nc.vector.memset(warm[:], 0.0)
-            nc.scalar.activation(out=warm[:, 4:5], in_=warm[:, 0:1], func=ACT.Tanh)
-
-        def setup3():
-            make_identity(nc, ident[:])
-
-        def setup4():
-            nc.gpsimd.memset(rows[:], 0.0)
-            make_identity(nc, ident16[:])
-
-        def load_rows():
-            nc.sync.dma_start(out=rows[0:8, :], in_=c.rearrange("(i p) -> i p", p=P))
-            nc.sync.dma_start(out=rows[8:12, :], in_=damp.rearrange("(i p) -> i p", p=P))
-
-        def consts_a():
-            nc.vector.tensor_copy(out=T[("g32",)][:], in_=T[("g4",)][:])
-
-        def consts_b():
-            bk = bank(("rowt",), "tr")
-            nc.tensor.transpose(bk[:].bitcast(BF16)[:, 0:P], rows[:], ident16[:])
-
-        def consts_c():
-            nc.scalar.copy(out=cn[:], in_=T[("rowt",)][:].bitcast(BF16)[:, 0:12])
-
-        def consts_d():
-            nc.vector.tensor_tensor(out=dc[:], in0=cn[:, 4:8], in1=cn[:, 8:12], op=ALU.mult)
 
         load_w(0, 0)
         load_z(0, 0)
+        c_slots = load_slots("c_slots", c)
+        g_slots = load_slots("g_slots", g)
+        b_slots = load_slots("b_slots", b1)
         load_z(0, 1)
         load_w(1, 0)
-        setup()
-        heat_setup()
-        setup2()
-        setup3()
         load_z(1, 0)
         load_w(0, 1)
-        heat(4)
-        setup4()
-        heat(0)
-        heat(1)
-        heat(2)
-        load_z(1, 1)
-        wb_turn(0, 0, 1)
         load_w(1, 1)
-        load_ctrl(1)
-        wa_lay(0, 0, 1, "v")
-        load_rows()
-        wa_lay(0, 0, 0, "v")
-        wb_turn(0, 0, 0)
-        wb_out(0, 0, 1)
-        consts_a()
-        heat(3)
-        wa_q(0, 0)
-        z_turn(0, 1, 0)
-        wb_out(0, 0, 0)
-        z_turn(0, 0, 1)
-        z_turn(0, 0, 0)
-        wb_q(0, 0)
-        x_mul(0, 1, 0)
-        wa_lay(1, 0, 0, "s")
+        load_z(1, 1)
+        nc.vector.memset(ones[:], 1.0)
+        quantize(("ones",), P)
+        nc.vector.memset(warm[:], 0.0)
+        nc.scalar.activation(out=warm[:, 4:5], in_=warm[:, 0:1], func=ACT.Tanh)
+        make_identity(nc, ident[:])
+        nc.gpsimd.memset(rows[:], 0.0)
+        make_identity(nc, ident16[:])
+        nc.sync.dma_start(out=rows[0 : 2 * BLOCKS, :], in_=c.rearrange("(i p) -> i p", p=P))
+        nc.sync.dma_start(out=rows[2 * BLOCKS : 3 * BLOCKS, :], in_=damp.rearrange("(i p) -> i p", p=P))
         load_ctrl(0)
+        load_ctrl(1)
+        nc.vector.tensor_copy(out=g32[:], in_=g_slots[:])
+        for k in range(4):
+            heat(k)
+
+        wa_lay(0, 0, 0, "scalar")
+        wa_lay(0, 0, 1, "vector")
+        wb_turn(0, 0, 0)
+        wb_turn(0, 0, 1)
+        z_turn(0, 1, 0)
+        heat(4)
+        heat(5)
+        wa_quant(0, 0)
+        wb_out(0, 0, 0)
+        wb_out(0, 0, 1)
+        x_mul(0, 1, 0)
+        wb_quant(0, 0)
+
+        z_turn(0, 0, 0)
+        z_turn(0, 0, 1)
         z_turn(0, 1, 1)
-        x_mul(0, 0, 1)
-        wb_turn(1, 0, 1)
-        wa_lay(1, 0, 1, "s")
+        heat(6)
         x_mul(0, 0, 0)
-        z_turn(1, 0, 0)
+        x_mul(0, 0, 1)
         x_mul(0, 1, 1)
-        x_q(0, 0)
-        z_turn(1, 1, 0)
-        x_q(0, 1)
-        wa_lay(0, 1, 0, "s")
-        wa_q(1, 0)
-        s1_mm(0, 0, 3)
-        wa_lay(0, 1, 1, "v")
-        wb_out(1, 0, 1)
-        x_mul(1, 0, 0)
-        z_turn(1, 0, 1)
-        s1_tanh(0, 0, 3)
-        wa_q(0, 1)
-        wa_lay(1, 1, 0, "s")
-        z_turn(1, 1, 1)
-        wb_turn(0, 1, 1)
-        x_mul(1, 1, 0)
-        s1_mm(0, 0, 0)
-        wb_out(0, 1, 1)
-        wa_lay(1, 1, 1, "v")
-        x_mul(1, 0, 1)
-        s1_mm(0, 0, 1)
-        wa_q(1, 1)
-        s1_tanh(0, 0, 0)
-        x_mul(1, 1, 1)
-        s1_mm(0, 0, 2)
-        s1_mm(0, 1, 3)
-        s1_mm(0, 1, 2)
-        s1_tanh(0, 0, 1)
-        x_q(1, 0)
-        s1_tanh(0, 0, 2)
-        s1_tanh(0, 1, 3)
-        x_q(1, 1)
-        wb_turn(0, 1, 0)
-        s1_tanh(0, 1, 2)
+        wa_lay(1, 0, 0, "scalar")
+        wa_lay(1, 0, 1, "scalar")
+        x_quant(0, 0)
+        x_quant(0, 1)
+        wa_quant(1, 0)
+
         wb_turn(1, 0, 0)
-        d_mul(0, 0)
-        wb_out(0, 1, 0)
+        wb_turn(1, 0, 1)
+        z_turn(1, 0, 0)
+        heat(7)
+        z_turn(1, 1, 0)
         wb_out(1, 0, 0)
-        s1_mm(0, 1, 1)
-        s1_mm(0, 1, 0)
-        s1_tanh(0, 1, 1)
-        wb_q(1, 0)
-        wb_turn(1, 1, 1)
-        s1_tanh(0, 1, 0)
-        d_q(0, 0)
-        consts_b()
+        wb_out(1, 0, 1)
+        wa_lay(0, 1, 0, "vector")
+        wa_lay(0, 1, 1, "scalar")
+        wb_quant(1, 0)
+        wa_lay(1, 1, 0, "vector")
+        wa_lay(1, 1, 1, "scalar")
+
+        m_mm(0, 0, 0)
+        m_mm(0, 0, 1)
+        m_mm(0, 0, 2)
+        x_mul(1, 0, 0)
+        wa_quant(0, 1)
+        x_mul(1, 1, 0)
+        wa_quant(1, 1)
+        z_turn(1, 1, 1)
         wb_turn(1, 1, 0)
-        consts_c()
-        d_mul(0, 1)
-        wb_out(1, 1, 1)
-        s1_mm(1, 0, 0)
+        z_turn(1, 0, 1)
+        m_mm(0, 0, 3)
+
+        m_tanh(0, 0, 0)
+        m_tanh(0, 0, 1)
+        m_tanh(0, 0, 2)
         wb_out(1, 1, 0)
-        s1_mm(1, 0, 2)
-        s1_tanh(1, 0, 0)
-        s1_tanh(1, 0, 2)
-        s1_mm(1, 0, 1)
-        s1_mm(1, 0, 3)
-        s1_tanh(1, 0, 1)
-        s1_mm(1, 1, 0)
-        wb_q(1, 1)
-        consts_d()
-        d_q(0, 1)
-        s1_tanh(1, 0, 3)
-        s1_mm(1, 1, 1)
-        wb_q(0, 1)
-        s1_tanh(1, 1, 0)
-        s1_mm(1, 1, 3)
-        d_mul(1, 0)
-        s1_tanh(1, 1, 1)
-        s1_mm(1, 1, 2)
-        s1_tanh(1, 1, 3)
-        s2_mm(0, 1, 0)
-        s1_tanh(1, 1, 2)
-        s2_mm(0, 1, 2)
-        s2_hp(0, 0)
-        d_mul(1, 1)
-        s2_mm(0, 0, 0)
-        s2_hp(0, 2)
-        s2_mm(0, 1, 3)
-        s2_v(0, 0, "s")
-        s2_turn("hp", 0, 0)
-        s2_v(0, 2, "s")
-        s2_turn("hp", 0, 2)
-        s2_mm(0, 1, 1)
-        s2_stt(0, 0)
-        s2_mm(0, 0, 2)
-        d_q(1, 1)
-        s2_dq(0, 0, "s")
-        s2_mm(0, 0, 3)
-        s2_hp(0, 3)
-        s2_hp(0, 1)
-        s2_turn("wv", 0, 0)
-        s2_v(0, 3, "v")
-        s2_turn("hp", 0, 3)
-        s2_stt(0, 2)
-        s2_dq(0, 2, "s")
-        s2_turn("hp", 0, 1)
-        s2_stt(0, 3)
-        s2_v(0, 1, "s")
-        s2_turn("wv", 0, 2)
-        d_q(1, 0)
-        s2_dq(0, 3, "s")
-        s2_mm(0, 0, 1)
-        s2_dp(0, 0)
-        s2_dq(0, 1, "s")
-        s2_stt(0, 1)
-        s2_mm(1, 1, 3)
-        y_lay(0, 256, 512, "s")
-        y_store(0, 0, 512)
-        s2_turn("wv", 0, 3)
-        s2_dp(0, 2)
-        s2_turn("wv", 0, 1)
-        s2_mm(1, 0, 3)
-        s2_dp(0, 3)
-        s2_hp(1, 3)
-        s2_dp(0, 1)
-        s2_mm(1, 1, 1)
-        s2_v(1, 3, "s")
-        y_lay(0, 0, 256, "v")
-        y_lay(0, 768, 1024, "s")
-        s2_mm(1, 1, 2)
-        y_store(0, 512, 1024)
-        s2_hp(1, 1)
-        s2_mm(1, 1, 0)
-        s2_stt(1, 3)
-        y_lay(0, 512, 768, "v")
-        y_q(0, 0, 512)
-        s2_turn("wv", 1, 3)
-        s2_turn("hp", 1, 3)
-        s2_hp(1, 0)
-        s2_turn("hp", 1, 1)
-        s2_dp(1, 3)
-        s2_hp(1, 2)
-        s2_turn("hp", 1, 0)
-        y_store(1, 896, 1024)
-        s2_dq(1, 1, "s")
-        y_q(0, 512, 1024)
-        s2_turn("hp", 1, 2)
-        s2_v(1, 2, "v")
-        s2_dq(1, 3, "s")
-        s_store(0, 0, "y")
-        s2_mm(1, 0, 2)
-        s2_v(1, 1, "v")
-        q_store(0, 0, 1024)
-        s2_dq(1, 2, "v")
-        s_store(0, 3, "y")
-        s_store(0, 1, "y")
-        s_store(0, 2, "y")
-        s2_mm(1, 0, 1)
-        s2_dq(1, 0, "s")
-        s2_stt(1, 2)
-        s2_v(1, 0, "s")
-        s2_mm(1, 0, 0)
-        s2_turn("wv", 1, 2)
-        y_store(1, 0, 512)
-        s2_stt(1, 1)
-        s2_turn("wv", 1, 1)
-        s2_stt(1, 0)
-        s2_dp(1, 2)
-        s2_turn("wv", 1, 0)
-        s2_dp(1, 1)
-        y_lay(1, 256, 512, "s")
-        y_lay(1, 0, 256, "s")
-        y_store(1, 768, 896)
-        s2_dp(1, 0)
-        y_lay(1, 512, 768, "s")
-        y_store(1, 512, 768)
-        y_lay(1, 768, 896, "v")
-        y_lay(1, 896, 1024, "v")
-        y_q(1, 0, 512)
-        q_store(1, 0, 512)
-        y_q(1, 896, 1024)
-        y_q(1, 768, 896)
-        y_q(1, 512, 768)
-        s_store(1, 3, "s")
-        q_store(1, 896, 1024)
-        s_store(1, 2, "s")
-        s_store(1, 0, "y")
-        q_store(1, 512, 896)
-        s_store(1, 1, "y")
+        m_tanh(0, 0, 3)
+        x_mul(1, 0, 1)
+        x_mul(1, 1, 1)
+        x_quant(1, 0)
+        x_quant(1, 1)
+
+        m_mm(0, 1, 0)
+        m_mm(0, 1, 1)
+        m_mm(0, 1, 2)
+        m_mm(0, 1, 3)
+        m_tanh(0, 1, 0)
+        m_tanh(0, 1, 1)
+        m_tanh(0, 1, 2)
+        m_tanh(0, 1, 3)
+        delta_mul(0, 0)
+
+        wb_turn(0, 1, 0)
+        rows_turned = bank(("rows_turned",), "turn")[:].bitcast(BF16)
+        nc.tensor.transpose(rows_turned[:, block(0)], rows[:], ident16[:])
+        wb_turn(1, 1, 1)
+        wb_turn(0, 1, 1)
+        wb_out(0, 1, 0)
+        wb_out(1, 1, 1)
+        wb_out(0, 1, 1)
+        delta_mul(0, 1)
+
+        m_mm(1, 0, 0)
+        m_mm(1, 0, 1)
+        m_mm(1, 0, 2)
+        m_mm(1, 0, 3)
+        m_tanh(1, 0, 0)
+        m_tanh(1, 0, 1)
+        m_tanh(1, 0, 2)
+        m_tanh(1, 0, 3)
+        nc.scalar.copy(out=cols[:], in_=rows_turned[:, 0 : 3 * BLOCKS])
+        delta_quant(0, 0)
+        wb_quant(1, 1)
+        delta_quant(0, 1)
+        wb_quant(0, 1)
+        nc.vector.tensor_tensor(out=damp_c[:], in0=cols[:, BLOCKS : 2 * BLOCKS], in1=cols[:, 2 * BLOCKS :], op=ALU.mult)
+        delta_mul(1, 0)
+
+        m_mm(1, 1, 0)
+        m_mm(1, 1, 1)
+        m_mm(1, 1, 2)
+        m_tanh(1, 1, 0)
+        m_tanh(1, 1, 1)
+        m_tanh(1, 1, 2)
+
+        r_mm(0, HI, 0)
+        r_mm(0, HI, 1)
+        r_mm(0, LO, 0)
+        hp_out(0, 0)
+        m_mm(1, 1, 3)
+        hp_out(0, 1)
+        damped(0, 0, "scalar")
+        m_tanh(1, 1, 3)
+        damped(0, 1, "gpsimd")
+        force(0, 0)
+        delta_mul(1, 1)
+
+        turn_back("hp", 0, 0)
+        turn_back("hp", 0, 1)
+        r_mm(0, HI, 2)
+        r_mm(0, HI, 3)
+        r_mm(0, LO, 1)
+        dq_out(0, 0, "scalar")
+        hp_out(0, 2)
+        hp_out(0, 3)
+        damped(0, 2, "scalar")
+        dq_out(0, 1, "scalar")
+        damped(0, 3, "scalar")
+        y_store(0, 0, 2)
+        delta_quant(1, 0)
+        delta_quant(1, 1)
+
+        turn_back("hp", 0, 2)
+        turn_back("fo", 0, 0)
+        turn_back("hp", 0, 3)
+        r_mm(0, LO, 2)
+        y_lay(0, 0, 2, "gpsimd")
+        force(0, 1)
+        r_mm(0, LO, 3)
+        dq_out(0, 2, "scalar")
+        dq_out(0, 3, "scalar")
+        y_store(0, 2, 4)
+        force(0, 2)
+        dp_out(0, 0)
+        r_mm(1, HI, 0)
+        turn_back("fo", 0, 1)
+        y_lay(0, 2, 4, "gpsimd")
+        force(0, 3)
+        dp_out(0, 1)
+        y_store(0, 4, 6)
+
+        hp_out(1, 0)
+        r_mm(1, HI, 1)
+        hp_out(1, 1)
+        damped(1, 0, "scalar")
+        turn_back("fo", 0, 2)
+        turn_back("fo", 0, 3)
+        turn_back("hp", 1, 0)
+        turn_back("hp", 1, 1)
+        dp_out(0, 2)
+        damped(1, 1, "gpsimd")
+        dp_out(0, 3)
+        y_store(0, 6, 8)
+        y_lay(0, 4, 6, "gpsimd")
+
+        r_mm(1, LO, 0)
+        r_mm(1, LO, 1)
+        dq_out(1, 0, "scalar")
+        dq_out(1, 1, "scalar")
+        y_store(1, 0, 2)
+        y_lay(0, 6, 8, "scalar")
+        force(1, 0)
+        force(1, 1)
+        r_mm(1, HI, 2)
+        r_mm(1, HI, 3)
+        y_quant(0, 0, 4)
+        y_quant(0, 4, 8)
+        codes_store(0, 0, 8)
+
+        turn_back("fo", 1, 0)
+        turn_back("fo", 1, 1)
+        hp_out(1, 2)
+        hp_out(1, 3)
+        damped(1, 2, "scalar")
+        r_mm(1, LO, 2)
+        dp_out(1, 0)
+        damped(1, 3, "gpsimd")
+        dp_out(1, 1)
+        y_store(1, 4, 6)
+        y_lay(1, 0, 2, "gpsimd")
+
+        turn_back("hp", 1, 2)
+        turn_back("hp", 1, 3)
+        force(1, 2)
+        r_mm(1, LO, 3)
+        dq_out(1, 2, "scalar")
+        dq_out(1, 3, "vector")
+        y_store(1, 2, 4)
+        y_lay(1, 4, 6, "scalar")
+        turn_back("fo", 1, 2)
+        force(1, 3)
+        dp_out(1, 2)
+        y_store(1, 6, 7)
+        y_lay(1, 2, 4, "scalar")
+        turn_back("fo", 1, 3)
+        y_quant(1, 4, 6)
+        y_lay(1, 6, 7, "gpsimd")
+        dp_out(1, 3)
+        y_store(1, 7, 8)
+        y_lay(1, 7, 8, "scalar")
+
+        y_quant(1, 0, 4)
+        codes_store(1, 0, 4)
+        y_quant(1, 6, 7)
+        y_quant(1, 7, 8)
+        scales_store(0, nc.sync)
+        scales_store(3, nc.scalar)
+        codes_store(1, 4, 8)
+        scales_store(2, nc.scalar)
+        scales_store(1, nc.sync)

from contextlib import ExitStack

import concourse.mybir as mybir
from concourse.masks import make_identity

F32 = mybir.dt.float32
BF16 = mybir.dt.bfloat16
I32 = mybir.dt.int32
U32 = mybir.dt.uint32
U8 = mybir.dt.uint8
FP8X4 = mybir.dt.float8_e4m3fn_x4
ALU = mybir.AluOpType
ACT = mybir.ActivationFunctionType

B, X, F = 1024, 1024, 1024
N = X // 2
P = 128
PACK = 4
GROUP = P * PACK
GROUPS = X // GROUP
BLOCKS = N // P
WORDS = GROUP // 2
LO, HI = 0, 1
FLOPS = 4 * B * X * F


def tile_porthamiltoniannetfield_x1_kernel(tc, z, ctrl, c, w1, g, b1, damp, out_0, out_1, out_2):
    nc = tc.nc
    with ExitStack() as ctx:
        keep = ctx.enter_context(tc.tile_pool(name="keep", bufs=1))
        work = ctx.enter_context(tc.tile_pool(name="work", bufs=2))
        psum = ctx.enter_context(tc.psum_pool(name="psum", bufs=4))
        ctx.enter_context(tc.manual_schedule())

        tiles = {}

        def label(key):
            return "_".join([str(part) for part in key])

        def kept(key, shape, dtype):
            tiles[key] = keep.tile(shape, dtype, name=label(key), align_bytes=64)
            return tiles[key]

        def staged(key, shape, dtype, bufs):
            if key not in tiles:
                tiles[key] = work.tile(shape, dtype, name=label(key), tag=key[0], bufs=bufs, align_bytes=64)
            return tiles[key]

        def bank(key, tag):
            tiles[key] = psum.tile([P, GROUP], F32, name=label(key), tag=tag)
            return tiles[key]

        def group(index):
            return slice(GROUP * index, GROUP * (index + 1))

        def block(index):
            return slice(P * index, P * (index + 1))

        def quantize(key, width):
            codes = kept(("codes",) + key, [P, width], U32)
            scales = kept(("scales",) + key, [P, width], U8)
            nc.vector.quantize_mx(out=codes[:].bitcast(FP8X4), scales=scales[:], in_=tiles[key][:])

        def mx_pass(out, lhs_key, lhs_cols, rhs_key, start, stop):
            nc.tensor.matmul_mx(
                out=out,
                lhsT=tiles[("codes",) + lhs_key][:, lhs_cols].bitcast(FP8X4),
                lhsT_scale=tiles[("scales",) + lhs_key][:, lhs_cols],
                rhs=tiles[("codes",) + rhs_key][:].bitcast(FP8X4),
                rhs_scale=tiles[("scales",) + rhs_key][:],
                start=start,
                stop=stop,
            )

        def copy_on(engine, out, in_):
            if engine == "vector":
                nc.vector.tensor_copy(out=out, in_=in_)
            else:
                nc.scalar.copy(out=out, in_=in_)

        def load_z(gb, h):
            if h == 0:
                kept(("z", gb), [P, PACK, X], BF16)
            rows = z[group(gb), :].rearrange("(p t) x -> p t x", t=PACK)
            nc.sync.dma_start(out=tiles[("z", gb)][:, 2 * h : 2 * h + 2, :], in_=rows[:, 2 * h : 2 * h + 2, :])

        def load_w(gx, gf):
            w = kept(("w", gx, gf), [P, PACK, GROUP], BF16)
            nc.sync.dma_start(out=w[:], in_=w1[group(gx), group(gf)].rearrange("(p j) f -> p j f", j=PACK))

        def load_ctrl(gb):
            u = kept(("ctrl", gb), [P, PACK, N], BF16)
            nc.sync.dma_start(out=u[:], in_=ctrl[group(gb), :].rearrange("(p t) n -> p t n", t=PACK))

        def load_slots(name, vec):
            slots = kept((name,), [P, GROUPS, PACK], BF16)
            nc.scalar.dma_start(out=slots[:], in_=vec.rearrange("(a p t) -> p a t", a=GROUPS, t=PACK))
            return slots

        def z_turn(gb, gx, h):
            turned = bank(("zt", gb, gx, h), "turn")
            words = tiles[("z", gb)][:].rearrange("p t x -> p (t x)").bitcast(F32)
            for u in range(2):
                for tt in range(2):
                    first = ((2 * h + tt) * GROUPS + gx) * WORDS
                    nc.tensor.transpose(turned[:, block(2 * u + tt)], words[:, first + u : first + WORDS : 2], ident[:])

        def x_mul(gb, gx, h):
            x = staged(("x", gb, gx), [P, GROUP * PACK], BF16, 2)
            half = GROUP * PACK // 2
            nc.vector.tensor_tensor(
                out=x[:, half * h : half * (h + 1)].rearrange("p (r u e) -> p r u e", u=2, e=2),
                in0=tiles[("zt", gb, gx, h)][:].bitcast(BF16).rearrange("p (u r e) -> p r u e", u=2, e=2),
                in1=c_slots[:, gx, :].rearrange("p (u e) -> p u e", e=2).unsqueeze(1).to_broadcast([P, 2 * P, 2, 2]),
                op=ALU.mult,
            )

        def x_quant(gb, gx):
            quantize(("x", gb, gx), GROUP)

        def wa_lay(gx, gf, h, engine):
            wa = staged(("wa", gx, gf), [P, GROUP * PACK], BF16, 3)
            pairs = slice(P // 4 * h, P // 4 * (h + 1))
            copy_on(
                engine,
                wa[:].rearrange("p (t a b j) -> p a t b j", t=PACK, b=2, j=PACK)[:, pairs],
                tiles[("w", gx, gf)][:].rearrange("p j (a b t) -> p a t b j", b=2, t=PACK)[:, pairs],
            )

        def wa_quant(gx, gf):
            quantize(("wa", gx, gf), GROUP)

        def wb_turn(gx, gf, h):
            turned = bank(("wt", gx, gf, h), "turn")
            words = tiles[("w", gx, gf)][:].rearrange("p j f -> p (j f)").bitcast(F32)
            for jj in range(2):
                for u in range(2):
                    first = (2 * h + jj) * WORDS
                    nc.tensor.transpose(turned[:, block(2 * jj + u)], words[:, first + u : first + WORDS : 2], ident[:])

        def wb_out(gx, gf, h):
            wb = staged(("wb", gx, gf), [P, GROUP * PACK], BF16, 2)
            nc.scalar.copy(
                out=wb[:].bitcast(F32).rearrange("p (r h q) -> p r h q", h=2, q=4)[:, :, h, :],
                in_=tiles[("wt", gx, gf, h)][:].rearrange("p (q r) -> p r q", q=4),
            )

        def wb_quant(gx, gf):
            quantize(("wb", gx, gf), GROUP)

        def m_mm(gb, gf, t):
            m = bank(("m", gb, gf, t), "sum")
            for gx in range(GROUPS):
                mx_pass(m[:], ("wa", gx, gf), block(t), ("x", gb, gx), gx == 0, gx == GROUPS - 1)

        def m_tanh(gb, gf, t):
            th = staged(("th", gb, gf), [P, PACK, GROUP], F32, 2)
            nc.scalar.activation(
                out=th[:, t, :],
                in_=tiles[("m", gb, gf, t)][:],
                func=ACT.Tanh,
                bias=b_slots[:, gf, t : t + 1],
                scale=g32[:, gf, t : t + 1],
            )

        def delta_mul(gb, gf):
            delta = staged(("delta", gb, gf), [P, GROUP * PACK], BF16, 2)
            nc.vector.tensor_tensor(
                out=delta[:].rearrange("p (c i t) -> p c t i", i=4, t=PACK),
                in0=tiles[("th", gb, gf)][:].rearrange("p t (c i) -> p c t i", i=4),
                in1=g32[:, gf, :].unsqueeze(1).unsqueeze(3).to_broadcast([P, GROUP // 4, PACK, 4]),
                op=ALU.mult,
            )

        def delta_quant(gb, gf):
            quantize(("delta", gb, gf), GROUP)

        def r_mm(gb, gx, i):
            r = bank(("r", gb, gx, i), "sum")
            for gf in range(GROUPS):
                mx_pass(r[:], ("wb", gx, gf), block(i), ("delta", gb, gf), gf == 0, gf == GROUPS - 1)

        def hp_out(gb, i):
            hp = staged(("hp", gb, i), [P, GROUP], F32, BLOCKS)
            nc.scalar.activation(out=hp[:], in_=tiles[("r", gb, HI, i)][:], func=ACT.Copy, scale=cols[:, BLOCKS + i : BLOCKS + i + 1])

        def damped(gb, i, engine):
            dh = staged(("dh", gb, i), [P, GROUP], F32, BLOCKS)
            if engine == "scalar":
                nc.scalar.activation(out=dh[:], in_=tiles[("r", gb, HI, i)][:], func=ACT.Copy, scale=damp_c[:, i : i + 1])
            else:
                factor = cols[:, 2 * BLOCKS + i : 2 * BLOCKS + i + 1]
                nc.gpsimd.tensor_scalar(out=dh[:], in0=tiles[("hp", gb, i)][:], scalar1=factor, scalar2=0.0, op0=ALU.mult, op1=ALU.add)

        def force(gb, i):
            fo = staged(("fo", gb, i), [P, GROUP], F32, BLOCKS)
            nc.vector.scalar_tensor_tensor(
                out=fo[:], in0=tiles[("r", gb, LO, i)][:], scalar=cols[:, i : i + 1], in1=tiles[("dh", gb, i)][:], op0=ALU.mult, op1=ALU.add
            )

        def turn_back(name, gb, i):
            turned = bank((name + "t", gb, i), "turn")
            for t in range(PACK):
                nc.tensor.transpose(turned[:, block(t)], tiles[(name, gb, i)][:, block(t)], ident[:])

        def dq_out(gb, i, engine):
            copy_on(engine, tiles[("y", gb)][:, :, block(i)], tiles[("hpt", gb, i)][:].rearrange("p (t n) -> p t n", t=PACK))

        def dp_out(gb, i):
            nc.vector.tensor_tensor(
                out=tiles[("y", gb)][:, :, block(BLOCKS + i)],
                in0=tiles[("ctrl", gb)][:, :, block(i)],
                in1=tiles[("fot", gb, i)][:].rearrange("p (t n) -> p t n", t=PACK),
                op=ALU.subtract,
            )

        def y_lay(gb, first, last, engine):
            laid = tiles[("y16", gb)][:, GROUP * first : GROUP * last]
            y = tiles[("y", gb)][:, :, P * first : P * last]
            if engine == "gpsimd":
                nc.gpsimd.tensor_scalar(
                    out=laid.rearrange("p (n t) -> p n t", t=PACK),
                    in0=y.rearrange("p t n -> p n t"),
                    scalar1=1.0,
                    scalar2=0.0,
                    op0=ALU.mult,
                    op1=ALU.add,
                )
            else:
                nc.scalar.copy(out=laid.rearrange("p (c i t) -> p c t i", i=4, t=PACK), in_=y.rearrange("p t (c i) -> p c t i", i=4))

        def y_quant(gb, first, last):
            nc.vector.quantize_mx(
                out=tiles[("y_codes", gb)][:, P * first : P * last].bitcast(FP8X4),
                scales=y_scales[:, gb, P * first : P * last],
                in_=tiles[("y16", gb)][:, GROUP * first : GROUP * last],
            )

        def y_store(gb, first, last):
            span = slice(P * first, P * last)
            nc.sync.dma_start(out=out_0[group(gb), span].rearrange("(p t) n -> p t n", t=PACK), in_=tiles[("y", gb)][:, :, span])

        def codes_store(gb, first, last):
            span = slice(P * first, P * last)
            words = out_1[gb].rearrange("p m t -> p (m t)").bitcast(I32)
            nc.sync.dma_start(out=words[:, span], in_=tiles[("y_codes", gb)][:, span].bitcast(I32))

        def scales_store(q, queue):
            queue.dma_start(
                out=out_2[:, 4 * q : 4 * q + 4, :].rearrange("a r m -> r a m").bitcast(I32),
                in_=y_scales[32 * q : 32 * q + 4, :, :].bitcast(I32),
            )

        def heat(k):
            idle = bank(("heat", k), "sum")
            for j in range(PACK):
                mx_pass(idle[:, block(j)], ("ones",), block(0), ("ones",), True, True)

        ident = kept(("ident",), [P, P], F32)
        ident16 = kept(("ident16",), [P, P], BF16)
        warm = kept(("warm",), [P, 8], F32)
        ones = kept(("ones",), [P, GROUP], BF16)
        g32 = kept(("g32",), [P, GROUPS, PACK], F32)
        rows = kept(("rows",), [P, P], BF16)
        cols = kept(("cols",), [P, 3 * BLOCKS], F32)
        damp_c = kept(("damp_c",), [P, BLOCKS], F32)
        y_scales = kept(("y_scales",), [P, GROUPS, X], U8)
        for gb in range(GROUPS):
            kept(("y", gb), [P, PACK, X], F32)
            kept(("y16", gb), [P, X * PACK], BF16)
            kept(("y_codes", gb), [P, X], U32)


        load_w(0, 0)
        load_z(0, 0)
        c_slots = load_slots("c_slots", c)
        g_slots = load_slots("g_slots", g)
        b_slots = load_slots("b_slots", b1)
        load_z(0, 1)
        load_w(1, 0)
        load_z(1, 0)
        load_w(0, 1)
        load_w(1, 1)
        load_z(1, 1)
        nc.vector.memset(ones[:], 1.0)
        quantize(("ones",), P)
        nc.vector.memset(warm[:], 0.0)
        nc.scalar.activation(out=warm[:, 4:5], in_=warm[:, 0:1], func=ACT.Tanh)
        make_identity(nc, ident[:])
        nc.gpsimd.memset(rows[:], 0.0)
        make_identity(nc, ident16[:])
        nc.sync.dma_start(out=rows[0 : 2 * BLOCKS, :], in_=c.rearrange("(i p) -> i p", p=P))
        nc.sync.dma_start(out=rows[2 * BLOCKS : 3 * BLOCKS, :], in_=damp.rearrange("(i p) -> i p", p=P))
        load_ctrl(0)
        load_ctrl(1)
        nc.vector.tensor_copy(out=g32[:], in_=g_slots[:])
        for k in range(4):
            heat(k)

        wa_lay(0, 0, 0, "scalar")
        wa_lay(0, 0, 1, "vector")
        wb_turn(0, 0, 0)
        wb_turn(0, 0, 1)
        z_turn(0, 1, 0)
        heat(4)
        heat(5)
        wa_quant(0, 0)
        wb_out(0, 0, 0)
        wb_out(0, 0, 1)
        x_mul(0, 1, 0)
        wb_quant(0, 0)

        z_turn(0, 0, 0)
        z_turn(0, 0, 1)
        z_turn(0, 1, 1)
        heat(6)
        x_mul(0, 0, 0)
        x_mul(0, 0, 1)
        x_mul(0, 1, 1)
        wa_lay(1, 0, 0, "scalar")
        wa_lay(1, 0, 1, "scalar")
        x_quant(0, 0)
        x_quant(0, 1)
        wa_quant(1, 0)

        wb_turn(1, 0, 0)
        wb_turn(1, 0, 1)
        z_turn(1, 0, 0)
        heat(7)
        z_turn(1, 1, 0)
        wb_out(1, 0, 0)
        wb_out(1, 0, 1)
        wa_lay(0, 1, 0, "vector")
        wa_lay(0, 1, 1, "scalar")
        wb_quant(1, 0)
        wa_lay(1, 1, 0, "vector")
        wa_lay(1, 1, 1, "scalar")

        m_mm(0, 0, 0)
        m_mm(0, 0, 1)
        m_mm(0, 0, 2)
        x_mul(1, 0, 0)
        wa_quant(0, 1)
        x_mul(1, 1, 0)
        wa_quant(1, 1)
        z_turn(1, 1, 1)
        wb_turn(1, 1, 0)
        z_turn(1, 0, 1)
        m_mm(0, 0, 3)

        m_tanh(0, 0, 0)
        m_tanh(0, 0, 1)
        m_tanh(0, 0, 2)
        wb_out(1, 1, 0)
        m_tanh(0, 0, 3)
        x_mul(1, 0, 1)
        x_mul(1, 1, 1)
        x_quant(1, 0)
        x_quant(1, 1)

        m_mm(0, 1, 0)
        m_mm(0, 1, 1)
        m_mm(0, 1, 2)
        m_mm(0, 1, 3)
        m_tanh(0, 1, 0)
        m_tanh(0, 1, 1)
        m_tanh(0, 1, 2)
        m_tanh(0, 1, 3)
        delta_mul(0, 0)

        wb_turn(0, 1, 0)
        rows_turned = bank(("rows_turned",), "turn")[:].bitcast(BF16)
        nc.tensor.transpose(rows_turned[:, block(0)], rows[:], ident16[:])
        wb_turn(1, 1, 1)
        wb_turn(0, 1, 1)
        wb_out(0, 1, 0)
        wb_out(1, 1, 1)
        wb_out(0, 1, 1)
        delta_mul(0, 1)

        m_mm(1, 0, 0)
        m_mm(1, 0, 1)
        m_mm(1, 0, 2)
        m_mm(1, 0, 3)
        m_tanh(1, 0, 0)
        m_tanh(1, 0, 1)
        m_tanh(1, 0, 2)
        m_tanh(1, 0, 3)
        nc.scalar.copy(out=cols[:], in_=rows_turned[:, 0 : 3 * BLOCKS])
        delta_quant(0, 0)
        wb_quant(1, 1)
        delta_quant(0, 1)
        wb_quant(0, 1)
        nc.vector.tensor_tensor(out=damp_c[:], in0=cols[:, BLOCKS : 2 * BLOCKS], in1=cols[:, 2 * BLOCKS :], op=ALU.mult)
        delta_mul(1, 0)

        m_mm(1, 1, 0)
        m_mm(1, 1, 1)
        m_mm(1, 1, 2)
        m_tanh(1, 1, 0)
        m_tanh(1, 1, 1)
        m_tanh(1, 1, 2)

        r_mm(0, HI, 0)
        r_mm(0, HI, 1)
        r_mm(0, LO, 0)
        hp_out(0, 0)
        m_mm(1, 1, 3)
        hp_out(0, 1)
        damped(0, 0, "scalar")
        m_tanh(1, 1, 3)
        damped(0, 1, "gpsimd")
        force(0, 0)
        delta_mul(1, 1)

        turn_back("hp", 0, 0)
        turn_back("hp", 0, 1)
        r_mm(0, HI, 2)
        r_mm(0, HI, 3)
        r_mm(0, LO, 1)
        dq_out(0, 0, "scalar")
        hp_out(0, 2)
        hp_out(0, 3)
        damped(0, 2, "scalar")
        dq_out(0, 1, "scalar")
        damped(0, 3, "scalar")
        y_store(0, 0, 2)
        delta_quant(1, 0)
        delta_quant(1, 1)

        turn_back("hp", 0, 2)
        turn_back("fo", 0, 0)
        turn_back("hp", 0, 3)
        r_mm(0, LO, 2)
        y_lay(0, 0, 2, "gpsimd")
        force(0, 1)
        r_mm(0, LO, 3)
        dq_out(0, 2, "scalar")
        dq_out(0, 3, "scalar")
        y_store(0, 2, 4)
        force(0, 2)
        dp_out(0, 0)
        r_mm(1, HI, 0)
        turn_back("fo", 0, 1)
        y_lay(0, 2, 4, "gpsimd")
        force(0, 3)
        dp_out(0, 1)
        y_store(0, 4, 6)

        hp_out(1, 0)
        r_mm(1, HI, 1)
        hp_out(1, 1)
        damped(1, 0, "scalar")
        turn_back("fo", 0, 2)
        turn_back("fo", 0, 3)
        turn_back("hp", 1, 0)
        turn_back("hp", 1, 1)
        dp_out(0, 2)
        damped(1, 1, "gpsimd")
        dp_out(0, 3)
        y_store(0, 6, 8)
        y_lay(0, 4, 6, "gpsimd")

        r_mm(1, LO, 0)
        r_mm(1, LO, 1)
        dq_out(1, 0, "scalar")
        dq_out(1, 1, "scalar")
        y_store(1, 0, 2)
        y_lay(0, 6, 8, "scalar")
        force(1, 0)
        force(1, 1)
        r_mm(1, HI, 2)
        r_mm(1, HI, 3)
        y_quant(0, 0, 4)
        y_quant(0, 4, 8)
        codes_store(0, 0, 8)

        turn_back("fo", 1, 0)
        turn_back("fo", 1, 1)
        hp_out(1, 2)
        hp_out(1, 3)
        damped(1, 2, "scalar")
        r_mm(1, LO, 2)
        dp_out(1, 0)
        damped(1, 3, "gpsimd")
        dp_out(1, 1)
        y_store(1, 4, 6)
        y_lay(1, 0, 2, "gpsimd")

        turn_back("hp", 1, 2)
        turn_back("hp", 1, 3)
        force(1, 2)
        r_mm(1, LO, 3)
        dq_out(1, 2, "scalar")
        dq_out(1, 3, "vector")
        y_store(1, 2, 4)
        y_lay(1, 4, 6, "scalar")
        turn_back("fo", 1, 2)
        force(1, 3)
        dp_out(1, 2)
        y_store(1, 6, 7)
        y_lay(1, 2, 4, "scalar")
        turn_back("fo", 1, 3)
        y_quant(1, 4, 6)
        y_lay(1, 6, 7, "gpsimd")
        dp_out(1, 3)
        y_store(1, 7, 8)
        y_lay(1, 7, 8, "scalar")

        y_quant(1, 0, 4)
        codes_store(1, 0, 4)
        y_quant(1, 6, 7)
        y_quant(1, 7, 8)
        scales_store(0, nc.sync)
        scales_store(3, nc.scalar)
        codes_store(1, 4, 8)
        scales_store(2, nc.scalar)
        scales_store(1, nc.sync)
